import numpy as np
import ml_dtypes


def mxq(x, axis, fmt="e4m3"):
    dtype, down = {"e4m3": (ml_dtypes.float8_e4m3fn, 7), "e5m2": (ml_dtypes.float8_e5m2, 14)}[fmt]
    v = np.moveaxis(np.asarray(x, np.float32).astype(ml_dtypes.bfloat16).astype(np.float64), axis, -1)
    blocks = v.reshape(v.shape[:-1] + (-1, 32))
    amax = np.abs(blocks).max(-1, keepdims=True)
    byte = np.maximum(np.where(amax > 0, np.frexp(amax)[1] - 1 + 127, 0) - down, 1)
    scale = np.exp2(byte - 127.0)
    codes = (blocks / scale).astype(np.float32).astype(dtype).astype(np.float64)
    return np.moveaxis((codes * scale).reshape(v.shape), -1, axis)


WIDE = False


def mx_kscale(k):
    if not WIDE:
        return np.ones(k)
    levels = np.array([18, -18])
    if k % 512:
        return np.exp2(np.random.permutation(np.resize(levels, k // 32))).repeat(32)
    a = np.empty((k // 512, 16))
    for p in range(k // 512):
        a[p, :8] = np.random.permutation(np.resize(levels, 8))
        for g in range(8):
            far = levels[np.abs(levels - a[p, g]) >= 10]
            a[p, g + 8] = far[np.random.randint(len(far))]
    return np.exp2(a.ravel()).repeat(32)


def f64(x):
    return np.asarray(x).astype(np.float64)


def striped(idx):
    return np.tile(np.asarray(idx).reshape(-1, 16).T, (8, 1)).astype(np.uint16)


def unstriped(offs):
    return offs[:16].T.reshape(-1).astype(np.int64)


def eight(idx):
    return np.concatenate([idx[h].reshape(-1, 16).T for h in range(8)]).astype(np.uint16)


def uneight(offs):
    return np.stack([offs[16 * h:16 * h + 16].T.reshape(-1) for h in range(8)]).astype(np.int64)

def planes(y):
    n, m = y.shape
    v = y.astype(np.float32).astype(ml_dtypes.bfloat16).astype(np.float64).reshape(n // 32, 32, m)
    top = np.abs(v).max(1)
    byte = np.clip(np.where(top > 0, np.frexp(top)[1] - 1 + 127 - 7, 1), 1, 254)
    codes = (v * np.exp2(127.0 - byte)[:, None, :]).reshape(n, m).astype(np.float32).astype(ml_dtypes.float8_e4m3fn).view(np.uint8)
    words = codes.reshape(n // 512, 128, 4, m).transpose(0, 1, 3, 2)
    return np.ascontiguousarray(words), np.ascontiguousarray(byte.astype(np.uint8).reshape(n // 512, 16, m))


def setup_inputs():
    n = np.random.standard_normal
    uni = np.random.uniform
    idx = np.stack([np.random.permutation(2048)[:512] for _ in range(8)])
    f_f = mx_kscale(512)
    return {
        "W": (n((512, 512)) / np.sqrt(512) * f_f[:, None]).astype(np.float32),
        "dz": (n((512, 512)) / f_f[:, None]).astype(np.float32),
        "eT": (n((512, 2048))).astype(np.float32),
        "cd": (uni(0.75, 1.3, (512, 1))).astype(np.float32),
        "offs": eight(idx),
    }


def reference(W, dz, eT, cd, offs):
    idx = uneight(offs)
    de = mxq(f64(W), 0, "e4m3").T @ mxq(f64(dz), 0, "e5m2")
    e_ = np.concatenate([f64(eT)[64 * run:64 * run + 64][:, idx[run % 8]] for run in range(8)])
    th = np.tanh(e_)
    g = f64(cd) * de * (1.0 - np.square(th))
    out_0 = np.zeros((512, 2048))
    for run in range(8):
        out_0[64 * run:64 * run + 64][:, idx[run % 8]] = g[64 * run:64 * run + 64]
    return (out_0,) + planes(out_0)

@@ -1,0 +1,156 @@
+from contextlib import ExitStack
+
+import concourse.mybir as mybir
+
+F32 = mybir.dt.float32
+BF16 = mybir.dt.bfloat16
+I32 = mybir.dt.int32
+U32 = mybir.dt.uint32
+U16 = mybir.dt.uint16
+U8 = mybir.dt.uint8
+E4M3 = mybir.dt.float8_e4m3fn_x4
+E5M2 = mybir.dt.float8_e5m2_x4
+ACT = mybir.ActivationFunctionType
+ALU = mybir.AluOpType
+
+P = 128
+LANES = 4
+ITEMS = 512
+FEATURES = 512
+COLUMNS = 2048
+CHUNK = 512
+FLOPS = 2 * 512 * 512 * 512
+
+
+def tile_attend_ghash_tnh_pl_kernel(tc, W, dz, eT, cd, offs, out_0, out_1, out_2):
+    nc = tc.nc
+    with ExitStack() as ctx:
+        keep = ctx.enter_context(tc.tile_pool(name="keep", bufs=1))
+        psum = ctx.enter_context(tc.psum_pool(name="psum", bufs=1))
+
+        offsets = keep.tile([P, ITEMS // 16], U16, name="offsets")
+        weights = keep.tile([P, LANES], F32, name="weights")
+        dz_raw = keep.tile([P, LANES, ITEMS], F32, name="dz_raw")
+        w_raw = [keep.tile([P, 2, FEATURES], F32, name="w_raw%d" % h) for h in range(2)]
+        table = [keep.tile([P, COLUMNS], F32, name="table%d" % t) for t in range(LANES)]
+        result = [keep.tile([P, COLUMNS], F32, name="result%d" % t) for t in range(LANES)]
+
+        eT_rows = eT.rearrange("(p t) c -> p t c", t=LANES)
+        out_rows = out_0.rearrange("(p t) c -> p t c", t=LANES)
+        w_rows = W.rearrange("(p j) d -> p j d", j=LANES)
+
+        nc.sync.dma_start(out=dz_raw[:], in_=dz.rearrange("(p j) i -> p j i", j=LANES))
+        nc.sync.dma_start(offsets[:], offs)
+        nc.sync.dma_start(out=table[0][:], in_=eT_rows[:, 0, :])
+        nc.sync.dma_start(out=w_raw[0][:], in_=w_rows[:, 0:2, :])
+        nc.sync.dma_start(out=w_raw[1][:], in_=w_rows[:, 2:4, :])
+        nc.scalar.dma_start(out=weights[:], in_=cd.rearrange("(p t) o -> p (t o)", t=LANES))
+        for t in range(1, LANES):
+            nc.sync.dma_start(out=table[t][:], in_=eT_rows[:, t, :])
+
+        for t in range(LANES):
+            nc.vector.memset(result[t][:].bitcast(I32), 0)
+
+        dz_bf = keep.tile([P, ITEMS, LANES], BF16, name="dz_bf", align_bytes=64)
+        dz_codes = keep.tile([P, ITEMS], U32, name="dz_codes", align_bytes=64)
+        dz_scales = keep.tile([P, ITEMS], U8, name="dz_scales", align_bytes=64)
+        nc.vector.tensor_copy(
+            out=dz_bf[:].rearrange("p (c i) j -> p c j i", i=4),
+            in_=dz_raw[:].rearrange("p j (c i) -> p c j i", i=4),
+        )
+        nc.vector.quantize_mx(
+            out=dz_codes[:].bitcast(E5M2), scales=dz_scales[:], in_=dz_bf[:].rearrange("p i j -> p (i j)")
+        )
+
+        w_bf = keep.tile([P, LANES, P, LANES], BF16, name="w_bf", align_bytes=64)
+        w_codes = [
+            keep.tile([P, P], U32, name="w_codes0", align_bytes=64),
+            keep.tile([P, P], U32, name="w_codes1", tag="turn1", align_bytes=64),
+            keep.tile([P, 2 * P], U32, name="w_codes23", align_bytes=64),
+        ]
+        w_plane = [w_codes[0][:], w_codes[1][:], w_codes[2][:, 0:P], w_codes[2][:, P : 2 * P]]
+        w_scales = keep.tile([P, FEATURES], U8, name="w_scales", align_bytes=64)
+        for h in range(2):
+            nc.vector.tensor_copy(
+                out=w_bf[:, :, :, 2 * h : 2 * h + 2].rearrange("p t m j -> p m j t"),
+                in_=w_raw[h][:].rearrange("p j (m t) -> p m j t", t=LANES),
+            )
+        w_flat = w_bf[:].rearrange("p t m j -> p (t m j)")
+        for part, (first, last) in enumerate(((0, 1), (1, 2), (2, 4))):
+            nc.vector.quantize_mx(
+                out=w_codes[part][:].bitcast(E4M3),
+                scales=w_scales[:, first * P : last * P],
+                in_=w_flat[:, first * P * LANES : last * P * LANES],
+            )
+
+        for t in range(LANES):
+            sums = psum.tile([P, ITEMS], F32, name="sums%d" % t)
+            nc.tensor.matmul_mx(
+                out=sums[:],
+                lhsT=w_plane[t].bitcast(E4M3),
+                lhsT_scale=w_scales[:, t * P : (t + 1) * P],
+                rhs=dz_codes[:].bitcast(E5M2),
+                rhs_scale=dz_scales[:],
+                start=True,
+                stop=True,
+            )
+            sig = keep.tile([P, ITEMS], F32, name="sig%d" % t, tag="turn%d" % t, align_bytes=64)
+            tanh2 = keep.tile([P, ITEMS], F32, name="tanh2_%d" % t, tag="turn%d" % (t + 1) if t > 0 else "first", align_bytes=64)
+            slope = keep.tile([P, ITEMS], F32, name="slope%d" % t)
+            scaled = keep.tile([P, ITEMS], F32, name="scaled%d" % t)
+            nc.scalar.activation(out=sig[:], in_=table[t][:].indirect(offsets[:]), func=ACT.Sigmoid, scale=2.0)
+            nc.scalar.activation(out=tanh2[:], in_=sig[:], func=ACT.Square, scale=2.0, bias=-1.0)
+            nc.scalar.activation(out=scaled[:], in_=sums[:], func=ACT.Copy, scale=weights[:, t : t + 1])
+            nc.scalar.activation(out=slope[:], in_=tanh2[:], func=ACT.Identity, scale=-1.0, bias=1.0)
+            nc.vector.tensor_tensor(result[t][:].indirect(offsets[:]), scaled[:], slope[:], ALU.mult)
+            nc.sync.dma_start(out=out_rows[:, t, :], in_=result[t][:])
+
+        rounded = keep.tile([P, LANES * COLUMNS], BF16, name="rounded", tag="turn4", align_bytes=64)
+        woven = keep.tile([P, COLUMNS, LANES], BF16, name="woven", align_bytes=64)
+        codes = keep.tile([P, COLUMNS], U32, name="codes", align_bytes=64)
+        scales = keep.tile([P, COLUMNS], U8, name="scales", align_bytes=64)
+        words_out = out_1[0].rearrange("p c l -> p (c l)").bitcast(I32)
+        scales_out = out_2[0].bitcast(I32)
+
+        def planes_of(c):
+            return rounded[:, c * LANES * CHUNK : (c + 1) * LANES * CHUNK].rearrange("p (t c) -> p t c", t=LANES)
+
+        def span_of(c):
+            return slice(c * CHUNK, (c + 1) * CHUNK)
+
+        def cast(engine_copy, t, c):
+            engine_copy(out=planes_of(c)[:, t, :], in_=result[t][:, span_of(c)])
+
+        def weave(engine_copy, c):
+            engine_copy(
+                out=woven[:, span_of(c), :].rearrange("p (c i) t -> p c t i", i=4),
+                in_=planes_of(c).rearrange("p t (c i) -> p c t i", i=4),
+            )
+
+        def quantise(c):
+            span = span_of(c)
+            nc.vector.quantize_mx(
+                out=codes[:, span].bitcast(E4M3),
+                scales=scales[:, span],
+                in_=woven[:, span, :].rearrange("p c t -> p (c t)"),
+            )
+            nc.sync.dma_start(out=words_out[:, span], in_=codes[:, span].bitcast(I32))
+
+        last = LANES - 1
+        for c in range(4):
+            for t in range(last):
+                cast(nc.scalar.copy, t, c)
+        cast(nc.scalar.copy, last, 3)
+        weave(nc.scalar.copy, 3)
+        for c in range(3):
+            cast(nc.vector.tensor_copy, last, c)
+        weave(nc.vector.tensor_copy, 0)
+        weave(nc.vector.tensor_copy, 1)
+        quantise(0)
+        weave(nc.vector.tensor_copy, 2)
+        quantise(1)
+        quantise(2)
+        quantise(3)
+        for q in range(4):
+            queue = nc.sync if q % 2 == 0 else nc.scalar
+            queue.dma_start(out=scales_out[4 * q : 4 * q + 4, :], in_=scales[32 * q : 32 * q + 4, :].bitcast(I32))

@@ -28,32 +28,36 @@ def tile_attend_ghash_tnh_pl_kernel(tc, W, dz, eT, cd, offs, out_0, out_1, out_2
         keep = ctx.enter_context(tc.tile_pool(name="keep", bufs=1))
         psum = ctx.enter_context(tc.psum_pool(name="psum", bufs=1))
 
+        def tile(name, shape, dtype, tag=None):
+            return keep.tile(shape, dtype, name=name, tag=tag or name, align_bytes=64)
+
         offsets = keep.tile([P, ITEMS // 16], U16, name="offsets")
-        weights = keep.tile([P, LANES], F32, name="weights")
-        dz_raw = keep.tile([P, LANES, ITEMS], F32, name="dz_raw")
-        w_raw = [keep.tile([P, 2, FEATURES], F32, name="w_raw%d" % h) for h in range(2)]
-        table = [keep.tile([P, COLUMNS], F32, name="table%d" % t) for t in range(LANES)]
-        result = [keep.tile([P, COLUMNS], F32, name="result%d" % t) for t in range(LANES)]
+        weights = tile("weights", [P, LANES], F32)
+        dz_raw = tile("dz_raw", [P, LANES, ITEMS], F32)
+        w_raw = tile("w_raw", [P, LANES, FEATURES], F32)
+        table = [tile("table%d" % t, [P, COLUMNS], F32) for t in range(LANES)]
+        result = [tile("result%d" % t, [P, COLUMNS], F32) for t in range(2)]
 
         eT_rows = eT.rearrange("(p t) c -> p t c", t=LANES)
         out_rows = out_0.rearrange("(p t) c -> p t c", t=LANES)
-        w_rows = W.rearrange("(p j) d -> p j d", j=LANES)
 
         nc.sync.dma_start(out=dz_raw[:], in_=dz.rearrange("(p j) i -> p j i", j=LANES))
+        nc.sync.dma_start(out=w_raw[:], in_=W.rearrange("(p j) d -> p j d", j=LANES))
         nc.sync.dma_start(offsets[:], offs)
-        nc.sync.dma_start(out=table[0][:], in_=eT_rows[:, 0, :])
-        nc.sync.dma_start(out=w_raw[0][:], in_=w_rows[:, 0:2, :])
-        nc.sync.dma_start(out=w_raw[1][:], in_=w_rows[:, 2:4, :])
         nc.scalar.dma_start(out=weights[:], in_=cd.rearrange("(p t) o -> p (t o)", t=LANES))
-        for t in range(1, LANES):
+        for t in range(LANES):
             nc.sync.dma_start(out=table[t][:], in_=eT_rows[:, t, :])
 
-        for t in range(LANES):
+        warm = tile("warm", [P, 1], F32)
+        nc.scalar.activation(out=warm[:], in_=weights[:, 0:1], func=ACT.Sigmoid)
+        one = tile("one", [P, 1], F32, "pairs")
+        nc.vector.memset(one[:], 1.0)
+        for t in range(2):
             nc.vector.memset(result[t][:].bitcast(I32), 0)
 
-        dz_bf = keep.tile([P, ITEMS, LANES], BF16, name="dz_bf", align_bytes=64)
-        dz_codes = keep.tile([P, ITEMS], U32, name="dz_codes", align_bytes=64)
-        dz_scales = keep.tile([P, ITEMS], U8, name="dz_scales", align_bytes=64)
+        dz_bf = tile("dz_bf", [P, ITEMS, LANES], BF16)
+        dz_codes = tile("dz_codes", [P, ITEMS], U32, "clear3")
+        dz_scales = tile("dz_scales", [P, ITEMS], U8)
         nc.vector.tensor_copy(
             out=dz_bf[:].rearrange("p (c i) j -> p c j i", i=4),
             in_=dz_raw[:].rearrange("p j (c i) -> p c j i", i=4),
@@ -62,95 +66,125 @@ def tile_attend_ghash_tnh_pl_kernel(tc, W, dz, eT, cd, offs, out_0, out_1, out_2
             out=dz_codes[:].bitcast(E5M2), scales=dz_scales[:], in_=dz_bf[:].rearrange("p i j -> p (i j)")
         )
 
-        w_bf = keep.tile([P, LANES, P, LANES], BF16, name="w_bf", align_bytes=64)
-        w_codes = [
-            keep.tile([P, P], U32, name="w_codes0", align_bytes=64),
-            keep.tile([P, P], U32, name="w_codes1", tag="turn1", align_bytes=64),
-            keep.tile([P, 2 * P], U32, name="w_codes23", align_bytes=64),
-        ]
-        w_plane = [w_codes[0][:], w_codes[1][:], w_codes[2][:, 0:P], w_codes[2][:, P : 2 * P]]
-        w_scales = keep.tile([P, FEATURES], U8, name="w_scales", align_bytes=64)
+        w_codes = tile("w_codes", [P, FEATURES], U32)
+        w_scales = tile("w_scales", [P, FEATURES], U8)
+        w_dealt = w_raw[:].rearrange("p j (m t) -> p m j t", t=LANES)
+        w_bf = [tile("w_bf%d" % h, [P, 2, P, LANES], BF16) for h in range(2)]
+        for h, engine_copy in enumerate((nc.vector.tensor_copy, nc.scalar.copy)):
+            engine_copy(out=w_bf[h][:].rearrange("p t m j -> p m j t"), in_=w_dealt[:, :, :, 2 * h : 2 * h + 2])
         for h in range(2):
-            nc.vector.tensor_copy(
-                out=w_bf[:, :, :, 2 * h : 2 * h + 2].rearrange("p t m j -> p m j t"),
-                in_=w_raw[h][:].rearrange("p j (m t) -> p m j t", t=LANES),
-            )
-        w_flat = w_bf[:].rearrange("p t m j -> p (t m j)")
-        for part, (first, last) in enumerate(((0, 1), (1, 2), (2, 4))):
+            span = slice(2 * h * P, 2 * (h + 1) * P)
             nc.vector.quantize_mx(
-                out=w_codes[part][:].bitcast(E4M3),
-                scales=w_scales[:, first * P : last * P],
-                in_=w_flat[:, first * P * LANES : last * P * LANES],
+                out=w_codes[:, span].bitcast(E4M3),
+                scales=w_scales[:, span],
+                in_=w_bf[h][:].rearrange("p t m j -> p (t m j)"),
             )
 
+        sums = [psum.tile([P, ITEMS], F32, name="sums%d" % t) for t in range(LANES)]
         for t in range(LANES):
-            sums = psum.tile([P, ITEMS], F32, name="sums%d" % t)
             nc.tensor.matmul_mx(
-                out=sums[:],
-                lhsT=w_plane[t].bitcast(E4M3),
+                out=sums[t][:],
+                lhsT=w_codes[:, t * P : (t + 1) * P].bitcast(E4M3),
                 lhsT_scale=w_scales[:, t * P : (t + 1) * P],
                 rhs=dz_codes[:].bitcast(E5M2),
                 rhs_scale=dz_scales[:],
                 start=True,
                 stop=True,
             )
-            sig = keep.tile([P, ITEMS], F32, name="sig%d" % t, tag="turn%d" % t, align_bytes=64)
-            tanh2 = keep.tile([P, ITEMS], F32, name="tanh2_%d" % t, tag="turn%d" % (t + 1) if t > 0 else "first", align_bytes=64)
-            slope = keep.tile([P, ITEMS], F32, name="slope%d" % t)
-            scaled = keep.tile([P, ITEMS], F32, name="scaled%d" % t)
-            nc.scalar.activation(out=sig[:], in_=table[t][:].indirect(offsets[:]), func=ACT.Sigmoid, scale=2.0)
-            nc.scalar.activation(out=tanh2[:], in_=sig[:], func=ACT.Square, scale=2.0, bias=-1.0)
-            nc.scalar.activation(out=scaled[:], in_=sums[:], func=ACT.Copy, scale=weights[:, t : t + 1])
-            nc.scalar.activation(out=slope[:], in_=tanh2[:], func=ACT.Identity, scale=-1.0, bias=1.0)
-            nc.vector.tensor_tensor(result[t][:].indirect(offsets[:]), scaled[:], slope[:], ALU.mult)
+
+        side = tile("side", [P, 3 * LANES * CHUNK], F32)
+        side_planes = side[:].rearrange("p (g t c) -> p g t c", g=3, t=LANES)
+
+        def front(t):
+            return result[t][:, 0 : 3 * CHUNK].rearrange("p (g c) -> p g c", g=3)
+
+        scaled = [tile("scaled%d" % t, [P, ITEMS], F32) for t in range(2)]
+        slope = [tile("slope%d" % t, [P, ITEMS], F32) for t in range(LANES)]
+
+        sig = tile("sig0", [P, ITEMS], F32, "clear2")
+        nc.scalar.activation(out=sig[:], in_=table[0][:].indirect(offsets[:]), func=ACT.Sigmoid, scale=2.0)
+        nc.vector.tensor_scalar(scaled[0][:], sums[0][:], weights[:, 0:1], -4.0, ALU.mult, ALU.mult)
+        nc.vector.tensor_scalar(scaled[1][:], sums[1][:], weights[:, 1:2], None, ALU.mult)
+        late_scaled = tile("late_scaled", [P, 2 * ITEMS], F32, "table0")
+        scaled.extend([late_scaled[:, 0:ITEMS], late_scaled[:, ITEMS : 2 * ITEMS]])
+        for t in (2, 3):
+            nc.scalar.activation(out=scaled[t][:], in_=sums[t][:], func=ACT.Copy, scale=weights[:, t : t + 1])
+        nc.vector.scalar_tensor_tensor(slope[0][:], sig[:], 1.0, sig[:], ALU.subtract, ALU.mult)
+
+        for t in (2, 3):
+            result.append(tile("result%d" % t, [P, COLUMNS], F32, "clear%d" % t))
+            nc.gpsimd.memset(result[t][:], 0.0)
+
+        for t in range(LANES):
+            if t > 0:
+                sig = tile("sig%d" % t, [P, ITEMS], F32, "turn%d" % t)
+                if t < LANES - 1:
+                    tanh2 = tile("tanh2_%d" % t, [P, ITEMS], F32, "turn%d" % (t + 1))[:]
+                else:
+                    tanh2 = side_planes[:, 0, 2, :]
+                nc.scalar.activation(out=sig[:], in_=table[t][:].indirect(offsets[:]), func=ACT.Sigmoid, scale=2.0)
+                nc.scalar.activation(out=tanh2, in_=sig[:], func=ACT.Square, scale=2.0, bias=-1.0)
+                nc.scalar.activation(out=slope[t][:], in_=tanh2, func=ACT.Identity, scale=-1.0, bias=one[:])
+            nc.vector.tensor_tensor(result[t][:].indirect(offsets[:]), scaled[t][:], slope[t][:], ALU.mult)
+            if t < 2:
+                nc.sync.dma_start(out=side_planes[:, :, t, :], in_=front(t))
             nc.sync.dma_start(out=out_rows[:, t, :], in_=result[t][:])
 
-        rounded = keep.tile([P, LANES * COLUMNS], BF16, name="rounded", tag="turn4", align_bytes=64)
-        woven = keep.tile([P, COLUMNS, LANES], BF16, name="woven", align_bytes=64)
-        codes = keep.tile([P, COLUMNS], U32, name="codes", align_bytes=64)
-        scales = keep.tile([P, COLUMNS], U8, name="scales", align_bytes=64)
+        woven = [tile("woven%d" % c, [P, CHUNK, LANES], BF16) for c in range(4)]
+        codes = tile("codes", [P, COLUMNS], U32)
+        scales = tile("scales", [P, CHUNK], U8)
         words_out = out_1[0].rearrange("p c l -> p (c l)").bitcast(I32)
-        scales_out = out_2[0].bitcast(I32)
+        scales_out = out_2[0].bitcast(I32).rearrange("r (a c) -> a r c", a=4)
 
-        def planes_of(c):
-            return rounded[:, c * LANES * CHUNK : (c + 1) * LANES * CHUNK].rearrange("p (t c) -> p t c", t=LANES)
+        pairs = tile("pairs", [P, 2, CHUNK, 2], BF16)
 
-        def span_of(c):
-            return slice(c * CHUNK, (c + 1) * CHUNK)
-
-        def cast(engine_copy, t, c):
-            engine_copy(out=planes_of(c)[:, t, :], in_=result[t][:, span_of(c)])
+        def set_aside_last(engine_copy, c):
+            engine_copy(out=side_planes[:, c, 3, :], in_=result[3][:, c * CHUNK : (c + 1) * CHUNK])
 
         def weave(engine_copy, c):
             engine_copy(
-                out=woven[:, span_of(c), :].rearrange("p (c i) t -> p c t i", i=4),
-                in_=planes_of(c).rearrange("p t (c i) -> p c t i", i=4),
+                out=woven[c][:].rearrange("p (c i) t -> p c t i", i=4),
+                in_=side_planes[:, c, :, :].rearrange("p t (c i) -> p c t i", i=4),
             )
 
-        def quantise(c):
-            span = span_of(c)
+        def pair_up(t):
+            nc.scalar.copy(out=pairs[:, t // 2, :, t % 2], in_=result[t][:, 3 * CHUNK : COLUMNS])
+
+        def weave_pairs(first, last):
+            words_in = pairs[:].rearrange("p u c e -> p u (c e)").bitcast(F32)
+            words = woven[3][:].rearrange("p c t -> p (c t)").bitcast(F32).rearrange("p (c u) -> p c u", u=2)
+            nc.scalar.copy(out=words[:, first:last, :], in_=words_in[:, :, first:last].rearrange("p u c -> p c u"))
+
+        def quantise(c, first, last):
             nc.vector.quantize_mx(
-                out=codes[:, span].bitcast(E4M3),
-                scales=scales[:, span],
-                in_=woven[:, span, :].rearrange("p c t -> p (c t)"),
+                out=codes[:, c * CHUNK + first : c * CHUNK + last].bitcast(E4M3),
+                scales=scales[4 * c : P, first:last],
+                in_=woven[c][:, first:last, :].rearrange("p c t -> p (c t)"),
             )
-            nc.sync.dma_start(out=words_out[:, span], in_=codes[:, span].bitcast(I32))
 
-        last = LANES - 1
-        for c in range(4):
-            for t in range(last):
-                cast(nc.scalar.copy, t, c)
-        cast(nc.scalar.copy, last, 3)
-        weave(nc.scalar.copy, 3)
+        def store_words(queue, first, last):
+            queue.dma_start(out=words_out[:, first:last], in_=codes[:, first:last].bitcast(I32))
+
+        for t in range(3):
+            pair_up(t)
+        nc.scalar.copy(out=side_planes[:, :, 2, :], in_=front(2))
         for c in range(3):
-            cast(nc.vector.tensor_copy, last, c)
+            set_aside_last(nc.vector.tensor_copy if c < 2 else nc.scalar.copy, c)
+        pair_up(3)
         weave(nc.vector.tensor_copy, 0)
         weave(nc.vector.tensor_copy, 1)
-        quantise(0)
-        weave(nc.vector.tensor_copy, 2)
-        quantise(1)
-        quantise(2)
-        quantise(3)
+        weave(nc.scalar.copy, 2)
+        quantise(0, 0, CHUNK)
+        quantise(1, 0, CHUNK)
+        store_words(nc.sync, 0, 2 * CHUNK)
+        quantise(2, 0, CHUNK)
+        store_words(nc.sync, 2 * CHUNK, 3 * CHUNK)
+        weave_pairs(0, CHUNK // 2)
+        quantise(3, 0, CHUNK // 2)
+        store_words(nc.sync, 3 * CHUNK, 3 * CHUNK + CHUNK // 2)
+        weave_pairs(CHUNK // 2, CHUNK)
+        quantise(3, CHUNK // 2, CHUNK)
+        store_words(nc.scalar, 3 * CHUNK + CHUNK // 2, COLUMNS)
         for q in range(4):
             queue = nc.sync if q % 2 == 0 else nc.scalar
-            queue.dma_start(out=scales_out[4 * q : 4 * q + 4, :], in_=scales[32 * q : 32 * q + 4, :].bitcast(I32))
+            queue.dma_start(out=scales_out[:, 4 * q : 4 * q + 4, :], in_=scales[32 * q : 32 * q + 16, :].bitcast(I32))

@@ -121,13 +121,13 @@ def tile_attend_ghash_tnh_pl_kernel(tc, W, dz, eT, cd, offs, out_0, out_1, out_2
                 if t < LANES - 1:
                     tanh2 = tile("tanh2_%d" % t, [P, ITEMS], F32, "turn%d" % (t + 1))[:]
                 else:
-                    tanh2 = side_planes[:, 0, 2, :]
+                    tanh2 = side[:, 10 * CHUNK - ITEMS // 2 : 10 * CHUNK + ITEMS // 2]
                 nc.scalar.activation(out=sig[:], in_=table[t][:].indirect(offsets[:]), func=ACT.Sigmoid, scale=2.0)
                 nc.scalar.activation(out=tanh2, in_=sig[:], func=ACT.Square, scale=2.0, bias=-1.0)
                 nc.scalar.activation(out=slope[t][:], in_=tanh2, func=ACT.Identity, scale=-1.0, bias=one[:])
             nc.vector.tensor_tensor(result[t][:].indirect(offsets[:]), scaled[t][:], slope[t][:], ALU.mult)
             if t < 2:
-                nc.sync.dma_start(out=side_planes[:, :, t, :], in_=front(t))
+                nc.sync.dma_start(out=side_planes[:, 0 : 3 - t, t, :], in_=front(t)[:, 0 : 3 - t, :])
             nc.sync.dma_start(out=out_rows[:, t, :], in_=result[t][:])
 
         woven = [tile("woven%d" % c, [P, CHUNK, LANES], BF16) for c in range(4)]
@@ -165,8 +165,10 @@ def tile_attend_ghash_tnh_pl_kernel(tc, W, dz, eT, cd, offs, out_0, out_1, out_2
         def store_words(queue, first, last):
             queue.dma_start(out=words_out[:, first:last], in_=codes[:, first:last].bitcast(I32))
 
-        for t in range(3):
+        for t in range(2):
             pair_up(t)
+        nc.scalar.copy(out=side_planes[:, 2, 1, :], in_=front(1)[:, 2, :])
+        pair_up(2)
         nc.scalar.copy(out=side_planes[:, :, 2, :], in_=front(2))
         for c in range(3):
             set_aside_last(nc.vector.tensor_copy if c < 2 else nc.scalar.copy, c)

@@ -98,13 +98,12 @@ def tile_attend_ghash_tnh_pl_kernel(tc, W, dz, eT, cd, offs, out_0, out_1, out_2
         def front(t):
             return result[t][:, 0 : 3 * CHUNK].rearrange("p (g c) -> p g c", g=3)
 
-        scaled = [tile("scaled%d" % t, [P, ITEMS], F32) for t in range(2)]
+        scaled = [tile("scaled0", [P, ITEMS], F32), None]
         slope = [tile("slope%d" % t, [P, ITEMS], F32) for t in range(LANES)]
 
         sig = tile("sig0", [P, ITEMS], F32, "clear2")
         nc.scalar.activation(out=sig[:], in_=table[0][:].indirect(offsets[:]), func=ACT.Sigmoid, scale=2.0)
         nc.vector.tensor_scalar(scaled[0][:], sums[0][:], weights[:, 0:1], -4.0, ALU.mult, ALU.mult)
-        nc.vector.tensor_scalar(scaled[1][:], sums[1][:], weights[:, 1:2], None, ALU.mult)
         late_scaled = tile("late_scaled", [P, 2 * ITEMS], F32, "table0")
         scaled.extend([late_scaled[:, 0:ITEMS], late_scaled[:, ITEMS : 2 * ITEMS]])
         for t in (2, 3):
@@ -125,7 +124,15 @@ def tile_attend_ghash_tnh_pl_kernel(tc, W, dz, eT, cd, offs, out_0, out_1, out_2
                 nc.scalar.activation(out=sig[:], in_=table[t][:].indirect(offsets[:]), func=ACT.Sigmoid, scale=2.0)
                 nc.scalar.activation(out=tanh2, in_=sig[:], func=ACT.Square, scale=2.0, bias=-1.0)
                 nc.scalar.activation(out=slope[t][:], in_=tanh2, func=ACT.Identity, scale=-1.0, bias=one[:])
-            nc.vector.tensor_tensor(result[t][:].indirect(offsets[:]), scaled[t][:], slope[t][:], ALU.mult)
+            if t == 0:
+                nc.vector.tensor_tensor(result[t][:].indirect(offsets[:]), scaled[t][:], slope[t][:], ALU.mult)
+            else:
+                grad = tile("grad%d" % t, [P, ITEMS], F32)
+                if t == 1:
+                    nc.vector.scalar_tensor_tensor(grad[:], sums[t][:], weights[:, 1:2], slope[t][:], ALU.mult, ALU.mult)
+                else:
+                    nc.gpsimd.tensor_tensor(grad[:], scaled[t][:], slope[t][:], ALU.mult)
+                nc.vector.tensor_copy(result[t][:].indirect(offsets[:]), grad[:])
             if t < 2:
                 nc.sync.dma_start(out=side_planes[:, 0 : 3 - t, t, :], in_=front(t)[:, 0 : 3 - t, :])
             nc.sync.dma_start(out=out_rows[:, t, :], in_=result[t][:])

@@ -92,108 +92,114 @@ def tile_attend_ghash_tnh_pl_kernel(tc, W, dz, eT, cd, offs, out_0, out_1, out_2
                 stop=True,
             )
 
-        side = tile("side", [P, 3 * LANES * CHUNK], F32)
-        side_planes = side[:].rearrange("p (g t c) -> p g t c", g=3, t=LANES)
-
-        def front(t):
-            return result[t][:, 0 : 3 * CHUNK].rearrange("p (g c) -> p g c", g=3)
-
-        scaled = [tile("scaled0", [P, ITEMS], F32), None]
+        scaled = [tile("scaled%d" % t, [P, ITEMS], F32) for t in (0, 2)]
+        scaled.insert(1, None)
         slope = [tile("slope%d" % t, [P, ITEMS], F32) for t in range(LANES)]
 
         sig = tile("sig0", [P, ITEMS], F32, "clear2")
         nc.scalar.activation(out=sig[:], in_=table[0][:].indirect(offsets[:]), func=ACT.Sigmoid, scale=2.0)
         nc.vector.tensor_scalar(scaled[0][:], sums[0][:], weights[:, 0:1], -4.0, ALU.mult, ALU.mult)
-        late_scaled = tile("late_scaled", [P, 2 * ITEMS], F32, "table0")
-        scaled.extend([late_scaled[:, 0:ITEMS], late_scaled[:, ITEMS : 2 * ITEMS]])
-        for t in (2, 3):
-            nc.scalar.activation(out=scaled[t][:], in_=sums[t][:], func=ACT.Copy, scale=weights[:, t : t + 1])
+        nc.vector.tensor_scalar(scaled[2][:], sums[2][:], weights[:, 2:3], None, ALU.mult)
+        scaled.append(tile("scaled3", [P, ITEMS], F32, "table0"))
+        nc.scalar.activation(out=scaled[3][:], in_=sums[3][:], func=ACT.Copy, scale=weights[:, 3:4])
         nc.vector.scalar_tensor_tensor(slope[0][:], sig[:], 1.0, sig[:], ALU.subtract, ALU.mult)
 
         for t in (2, 3):
             result.append(tile("result%d" % t, [P, COLUMNS], F32, "clear%d" % t))
             nc.gpsimd.memset(result[t][:], 0.0)
 
+        front_pairs = [tile("front_pairs%d" % c, [P, 2, CHUNK, 2], BF16) for c in range(2)]
+
+        def unit_tile(name, tag):
+            unit = tile(name, [P, 1], F32, tag)
+            nc.gpsimd.memset(unit[:], 1.0)
+            return unit
+
+        def pool_round(c, t, unit):
+            source = result[t][:, c * CHUNK : (c + 1) * CHUNK]
+            nc.gpsimd.tensor_scalar(front_pairs[c][:, t // 2, :, t % 2], source, unit[:], -0.0, ALU.mult, ALU.add)
+
         for t in range(LANES):
             if t > 0:
                 sig = tile("sig%d" % t, [P, ITEMS], F32, "turn%d" % t)
-                if t < LANES - 1:
-                    tanh2 = tile("tanh2_%d" % t, [P, ITEMS], F32, "turn%d" % (t + 1))[:]
-                else:
-                    tanh2 = side[:, 10 * CHUNK - ITEMS // 2 : 10 * CHUNK + ITEMS // 2]
+                tanh2 = tile("tanh2_%d" % t, [P, ITEMS], F32, "turn%d" % (t + 1))
                 nc.scalar.activation(out=sig[:], in_=table[t][:].indirect(offsets[:]), func=ACT.Sigmoid, scale=2.0)
-                nc.scalar.activation(out=tanh2, in_=sig[:], func=ACT.Square, scale=2.0, bias=-1.0)
-                nc.scalar.activation(out=slope[t][:], in_=tanh2, func=ACT.Identity, scale=-1.0, bias=one[:])
+                nc.scalar.activation(out=tanh2[:], in_=sig[:], func=ACT.Square, scale=2.0, bias=-1.0)
+                nc.scalar.activation(out=slope[t][:], in_=tanh2[:], func=ACT.Identity, scale=-1.0, bias=one[:])
             if t == 0:
                 nc.vector.tensor_tensor(result[t][:].indirect(offsets[:]), scaled[t][:], slope[t][:], ALU.mult)
             else:
-                grad = tile("grad%d" % t, [P, ITEMS], F32)
+                grad = tile("grad%d" % t, [P, ITEMS], F32, {1: "grad1", 2: "grad2", 3: "slope2"}[t])
                 if t == 1:
                     nc.vector.scalar_tensor_tensor(grad[:], sums[t][:], weights[:, 1:2], slope[t][:], ALU.mult, ALU.mult)
                 else:
                     nc.gpsimd.tensor_tensor(grad[:], scaled[t][:], slope[t][:], ALU.mult)
                 nc.vector.tensor_copy(result[t][:].indirect(offsets[:]), grad[:])
-            if t < 2:
-                nc.sync.dma_start(out=side_planes[:, 0 : 3 - t, t, :], in_=front(t)[:, 0 : 3 - t, :])
             nc.sync.dma_start(out=out_rows[:, t, :], in_=result[t][:])
+            if t == 0:
+                unit = unit_tile("unit0", "grad2")
+                for c in range(2):
+                    pool_round(c, 0, unit)
+            if t == 2:
+                pool_round(0, 1, unit_tile("unit1", "slope2"))
+        unit = unit_tile("unit2", "slope3")
+        pool_round(1, 1, unit)
+        for c in range(2):
+            pool_round(c, 2, unit)
+        last_unit = unit_tile("unit3", "slope3")
 
         woven = [tile("woven%d" % c, [P, CHUNK, LANES], BF16) for c in range(4)]
         codes = tile("codes", [P, COLUMNS], U32)
-        scales = tile("scales", [P, CHUNK], U8)
+        scales = tile("scales", [P, 2 * CHUNK], U8)
         words_out = out_1[0].rearrange("p c l -> p (c l)").bitcast(I32)
-        scales_out = out_2[0].bitcast(I32).rearrange("r (a c) -> a r c", a=4)
+        scales_out = out_2[0].bitcast(I32).rearrange("r (a c) -> a r c", a=2)
 
-        pairs = tile("pairs", [P, 2, CHUNK, 2], BF16)
+        back_pairs = [tile("pairs", [P, 2, CHUNK, 2], BF16), tile("pairs3", [P, 2, CHUNK, 2], BF16, "turn4")]
 
-        def set_aside_last(engine_copy, c):
-            engine_copy(out=side_planes[:, c, 3, :], in_=result[3][:, c * CHUNK : (c + 1) * CHUNK])
+        def pair_up(c, t):
+            nc.scalar.copy(out=back_pairs[c - 2][:, t // 2, :, t % 2], in_=result[t][:, c * CHUNK : (c + 1) * CHUNK])
 
-        def weave(engine_copy, c):
+        def weave_pairs(engine_copy, dtype, pairs, start, c, first, last):
+            words_in = pairs[:].rearrange("p u c e -> p u (c e)").bitcast(dtype)
+            words = woven[c][:].rearrange("p c t -> p (c t)").bitcast(dtype).rearrange("p (c u) -> p c u", u=2)
             engine_copy(
-                out=woven[c][:].rearrange("p (c i) t -> p c t i", i=4),
-                in_=side_planes[:, c, :, :].rearrange("p t (c i) -> p c t i", i=4),
+                out=words[:, first:last, :],
+                in_=words_in[:, :, start + first : start + last].rearrange("p u c -> p c u"),
             )
-
-        def pair_up(t):
-            nc.scalar.copy(out=pairs[:, t // 2, :, t % 2], in_=result[t][:, 3 * CHUNK : COLUMNS])
-
-        def weave_pairs(first, last):
-            words_in = pairs[:].rearrange("p u c e -> p u (c e)").bitcast(F32)
-            words = woven[3][:].rearrange("p c t -> p (c t)").bitcast(F32).rearrange("p (c u) -> p c u", u=2)
-            nc.scalar.copy(out=words[:, first:last, :], in_=words_in[:, :, first:last].rearrange("p u c -> p c u"))
 
         def quantise(c, first, last):
             nc.vector.quantize_mx(
                 out=codes[:, c * CHUNK + first : c * CHUNK + last].bitcast(E4M3),
-                scales=scales[4 * c : P, first:last],
+                scales=scales[4 * (c // 2) : P, c % 2 * CHUNK + first : c % 2 * CHUNK + last],
                 in_=woven[c][:, first:last, :].rearrange("p c t -> p (c t)"),
             )
 
         def store_words(queue, first, last):
             queue.dma_start(out=words_out[:, first:last], in_=codes[:, first:last].bitcast(I32))
 
-        for t in range(2):
-            pair_up(t)
-        nc.scalar.copy(out=side_planes[:, 2, 1, :], in_=front(1)[:, 2, :])
-        pair_up(2)
-        nc.scalar.copy(out=side_planes[:, :, 2, :], in_=front(2))
-        for c in range(3):
-            set_aside_last(nc.vector.tensor_copy if c < 2 else nc.scalar.copy, c)
-        pair_up(3)
-        weave(nc.vector.tensor_copy, 0)
-        weave(nc.vector.tensor_copy, 1)
-        weave(nc.scalar.copy, 2)
+        for t in range(3):
+            for c in (2, 3):
+                pair_up(c, t)
+        for c in range(2):
+            nc.vector.tensor_scalar(
+                front_pairs[c][:, 1, :, 1], result[3][:, c * CHUNK : (c + 1) * CHUNK], last_unit[:], None, ALU.mult
+            )
+        pair_up(2, 3)
+        weave_pairs(nc.scalar.copy, F32, back_pairs[0], 0, 2, 0, CHUNK)
+        pair_up(3, 3)
+        for c in range(2):
+            weave_pairs(nc.vector.tensor_copy, I32, front_pairs[c], 0, c, 0, CHUNK)
         quantise(0, 0, CHUNK)
         quantise(1, 0, CHUNK)
         store_words(nc.sync, 0, 2 * CHUNK)
         quantise(2, 0, CHUNK)
         store_words(nc.sync, 2 * CHUNK, 3 * CHUNK)
-        weave_pairs(0, CHUNK // 2)
+        weave_pairs(nc.scalar.copy, F32, back_pairs[1], 0, 3, 0, CHUNK // 2)
         quantise(3, 0, CHUNK // 2)
         store_words(nc.sync, 3 * CHUNK, 3 * CHUNK + CHUNK // 2)
-        weave_pairs(CHUNK // 2, CHUNK)
+        weave_pairs(nc.scalar.copy, F32, back_pairs[1], 0, 3, CHUNK // 2, CHUNK)
         quantise(3, CHUNK // 2, CHUNK)
         store_words(nc.scalar, 3 * CHUNK + CHUNK // 2, COLUMNS)
         for q in range(4):
             queue = nc.sync if q % 2 == 0 else nc.scalar
-            queue.dma_start(out=scales_out[:, 4 * q : 4 * q + 4, :], in_=scales[32 * q : 32 * q + 16, :].bitcast(I32))
+            queue.dma_start(out=scales_out[:, 4 * q : 4 * q + 4, :], in_=scales[32 * q : 32 * q + 8, :].bitcast(I32))

@@ -19,6 +19,7 @@ ITEMS = 512
 FEATURES = 512
 COLUMNS = 2048
 CHUNK = 512
+ORDER = (0, 2, 1, 3)
 FLOPS = 2 * 512 * 512 * 512
 
 
@@ -36,7 +37,7 @@ def tile_attend_ghash_tnh_pl_kernel(tc, W, dz, eT, cd, offs, out_0, out_1, out_2
         dz_raw = tile("dz_raw", [P, LANES, ITEMS], F32)
         w_raw = tile("w_raw", [P, LANES, FEATURES], F32)
         table = [tile("table%d" % t, [P, COLUMNS], F32) for t in range(LANES)]
-        result = [tile("result%d" % t, [P, COLUMNS], F32) for t in range(2)]
+        result = {t: tile("result%d" % t, [P, COLUMNS], F32) for t in ORDER[:2]}
 
         eT_rows = eT.rearrange("(p t) c -> p t c", t=LANES)
         out_rows = out_0.rearrange("(p t) c -> p t c", t=LANES)
@@ -45,14 +46,14 @@ def tile_attend_ghash_tnh_pl_kernel(tc, W, dz, eT, cd, offs, out_0, out_1, out_2
         nc.sync.dma_start(out=w_raw[:], in_=W.rearrange("(p j) d -> p j d", j=LANES))
         nc.sync.dma_start(offsets[:], offs)
         nc.scalar.dma_start(out=weights[:], in_=cd.rearrange("(p t) o -> p (t o)", t=LANES))
-        for t in range(LANES):
+        for t in ORDER:
             nc.sync.dma_start(out=table[t][:], in_=eT_rows[:, t, :])
 
         warm = tile("warm", [P, 1], F32)
         nc.scalar.activation(out=warm[:], in_=weights[:, 0:1], func=ACT.Sigmoid)
         one = tile("one", [P, 1], F32, "pairs")
         nc.vector.memset(one[:], 1.0)
-        for t in range(2):
+        for t in ORDER[:2]:
             nc.vector.memset(result[t][:].bitcast(I32), 0)
 
         dz_bf = tile("dz_bf", [P, ITEMS, LANES], BF16)
@@ -81,7 +82,7 @@ def tile_attend_ghash_tnh_pl_kernel(tc, W, dz, eT, cd, offs, out_0, out_1, out_2
             )
 
         sums = [psum.tile([P, ITEMS], F32, name="sums%d" % t) for t in range(LANES)]
-        for t in range(LANES):
+        for t in (0, 1, 3, 2):
             nc.tensor.matmul_mx(
                 out=sums[t][:],
                 lhsT=w_codes[:, t * P : (t + 1) * P].bitcast(E4M3),
@@ -92,20 +93,19 @@ def tile_attend_ghash_tnh_pl_kernel(tc, W, dz, eT, cd, offs, out_0, out_1, out_2
                 stop=True,
             )
 
-        scaled = [tile("scaled%d" % t, [P, ITEMS], F32) for t in (0, 2)]
-        scaled.insert(1, None)
+        scaled = {t: tile("scaled%d" % t, [P, ITEMS], F32) for t in (0, 1, 3)}
         slope = [tile("slope%d" % t, [P, ITEMS], F32) for t in range(LANES)]
 
         sig = tile("sig0", [P, ITEMS], F32, "clear2")
         nc.scalar.activation(out=sig[:], in_=table[0][:].indirect(offsets[:]), func=ACT.Sigmoid, scale=2.0)
         nc.vector.tensor_scalar(scaled[0][:], sums[0][:], weights[:, 0:1], -4.0, ALU.mult, ALU.mult)
-        nc.vector.tensor_scalar(scaled[2][:], sums[2][:], weights[:, 2:3], None, ALU.mult)
-        scaled.append(tile("scaled3", [P, ITEMS], F32, "table0"))
-        nc.scalar.activation(out=scaled[3][:], in_=sums[3][:], func=ACT.Copy, scale=weights[:, 3:4])
+        for t in (1, 3):
+            nc.vector.tensor_scalar(scaled[t][:], sums[t][:], weights[:, t : t + 1], None, ALU.mult)
         nc.vector.scalar_tensor_tensor(slope[0][:], sig[:], 1.0, sig[:], ALU.subtract, ALU.mult)
 
-        for t in (2, 3):
-            result.append(tile("result%d" % t, [P, COLUMNS], F32, "clear%d" % t))
+        for turn in (2, 3):
+            t = ORDER[turn]
+            result[t] = tile("result%d" % t, [P, COLUMNS], F32, "clear%d" % turn)
             nc.gpsimd.memset(result[t][:], 0.0)
 
         front_pairs = [tile("front_pairs%d" % c, [P, 2, CHUNK, 2], BF16) for c in range(2)]
@@ -119,40 +119,42 @@ def tile_attend_ghash_tnh_pl_kernel(tc, W, dz, eT, cd, offs, out_0, out_1, out_2
             source = result[t][:, c * CHUNK : (c + 1) * CHUNK]
             nc.gpsimd.tensor_scalar(front_pairs[c][:, t // 2, :, t % 2], source, unit[:], -0.0, ALU.mult, ALU.add)
 
-        for t in range(LANES):
-            if t > 0:
-                sig = tile("sig%d" % t, [P, ITEMS], F32, "turn%d" % t)
-                tanh2 = tile("tanh2_%d" % t, [P, ITEMS], F32, "turn%d" % (t + 1))
+        for turn, t in enumerate(ORDER):
+            if turn > 0:
+                sig = tile("sig%d" % t, [P, ITEMS], F32, "turn%d" % turn)
+                tanh2 = tile("tanh2_%d" % t, [P, ITEMS], F32, "turn%d" % (turn + 1))
                 nc.scalar.activation(out=sig[:], in_=table[t][:].indirect(offsets[:]), func=ACT.Sigmoid, scale=2.0)
                 nc.scalar.activation(out=tanh2[:], in_=sig[:], func=ACT.Square, scale=2.0, bias=-1.0)
                 nc.scalar.activation(out=slope[t][:], in_=tanh2[:], func=ACT.Identity, scale=-1.0, bias=one[:])
-            if t == 0:
+            if turn == 0:
                 nc.vector.tensor_tensor(result[t][:].indirect(offsets[:]), scaled[t][:], slope[t][:], ALU.mult)
             else:
-                grad = tile("grad%d" % t, [P, ITEMS], F32, {1: "grad1", 2: "grad2", 3: "slope2"}[t])
-                if t == 1:
-                    nc.vector.scalar_tensor_tensor(grad[:], sums[t][:], weights[:, 1:2], slope[t][:], ALU.mult, ALU.mult)
+                grad = tile("grad%d" % t, [P, ITEMS], F32, {1: "grad2", 2: "grad1", 3: "slope1"}[turn])
+                if turn == 1:
+                    nc.vector.scalar_tensor_tensor(
+                        grad[:], sums[t][:], weights[:, t : t + 1], slope[t][:], ALU.mult, ALU.mult
+                    )
                 else:
                     nc.gpsimd.tensor_tensor(grad[:], scaled[t][:], slope[t][:], ALU.mult)
                 nc.vector.tensor_copy(result[t][:].indirect(offsets[:]), grad[:])
             nc.sync.dma_start(out=out_rows[:, t, :], in_=result[t][:])
-            if t == 0:
-                unit = unit_tile("unit0", "grad2")
+            if turn == 0:
+                unit = unit_tile("unit0", "grad1")
                 for c in range(2):
                     pool_round(c, 0, unit)
-            if t == 2:
-                pool_round(0, 1, unit_tile("unit1", "slope2"))
+            if turn == 2:
+                pool_round(0, 2, unit_tile("unit1", "slope1"))
         unit = unit_tile("unit2", "slope3")
-        pool_round(1, 1, unit)
+        pool_round(1, 2, unit)
         for c in range(2):
-            pool_round(c, 2, unit)
+            pool_round(c, 1, unit)
         last_unit = unit_tile("unit3", "slope3")
 
         woven = [tile("woven%d" % c, [P, CHUNK, LANES], BF16) for c in range(4)]
         codes = tile("codes", [P, COLUMNS], U32)
-        scales = tile("scales", [P, 2 * CHUNK], U8)
+        scales = tile("scales", [P, CHUNK], U8)
         words_out = out_1[0].rearrange("p c l -> p (c l)").bitcast(I32)
-        scales_out = out_2[0].bitcast(I32).rearrange("r (a c) -> a r c", a=2)
+        scales_out = out_2[0].bitcast(I32).rearrange("r (a c) -> a r c", a=4)
 
         back_pairs = [tile("pairs", [P, 2, CHUNK, 2], BF16), tile("pairs3", [P, 2, CHUNK, 2], BF16, "turn4")]
 
@@ -170,14 +172,14 @@ def tile_attend_ghash_tnh_pl_kernel(tc, W, dz, eT, cd, offs, out_0, out_1, out_2
         def quantise(c, first, last):
             nc.vector.quantize_mx(
                 out=codes[:, c * CHUNK + first : c * CHUNK + last].bitcast(E4M3),
-                scales=scales[4 * (c // 2) : P, c % 2 * CHUNK + first : c % 2 * CHUNK + last],
+                scales=scales[4 * c : P, first:last],
                 in_=woven[c][:, first:last, :].rearrange("p c t -> p (c t)"),
             )
 
         def store_words(queue, first, last):
             queue.dma_start(out=words_out[:, first:last], in_=codes[:, first:last].bitcast(I32))
 
-        for t in range(3):
+        for t in ORDER[:3]:
             for c in (2, 3):
                 pair_up(c, t)
         for c in range(2):
@@ -189,10 +191,14 @@ def tile_attend_ghash_tnh_pl_kernel(tc, W, dz, eT, cd, offs, out_0, out_1, out_2
         pair_up(3, 3)
         for c in range(2):
             weave_pairs(nc.vector.tensor_copy, I32, front_pairs[c], 0, c, 0, CHUNK)
-        quantise(0, 0, CHUNK)
-        quantise(1, 0, CHUNK)
-        store_words(nc.sync, 0, 2 * CHUNK)
-        quantise(2, 0, CHUNK)
+        quantise(0, 0, CHUNK // 2)
+        quantise(0, CHUNK // 2, CHUNK)
+        store_words(nc.sync, 0, CHUNK)
+        quantise(1, 0, CHUNK // 2)
+        quantise(1, CHUNK // 2, CHUNK)
+        store_words(nc.sync, CHUNK, 2 * CHUNK)
+        quantise(2, 0, CHUNK // 2)
+        quantise(2, CHUNK // 2, CHUNK)
         store_words(nc.sync, 2 * CHUNK, 3 * CHUNK)
         weave_pairs(nc.scalar.copy, F32, back_pairs[1], 0, 3, 0, CHUNK // 2)
         quantise(3, 0, CHUNK // 2)
@@ -202,4 +208,4 @@ def tile_attend_ghash_tnh_pl_kernel(tc, W, dz, eT, cd, offs, out_0, out_1, out_2
         store_words(nc.scalar, 3 * CHUNK + CHUNK // 2, COLUMNS)
         for q in range(4):
             queue = nc.sync if q % 2 == 0 else nc.scalar
-            queue.dma_start(out=scales_out[:, 4 * q : 4 * q + 4, :], in_=scales[32 * q : 32 * q + 8, :].bitcast(I32))
+            queue.dma_start(out=scales_out[:, 4 * q : 4 * q + 4, :], in_=scales[32 * q : 32 * q + 16, :].bitcast(I32))

@@ -19,7 +19,7 @@ ITEMS = 512
 FEATURES = 512
 COLUMNS = 2048
 CHUNK = 512
-ORDER = (0, 2, 1, 3)
+ORDER = (2, 0, 1, 3)
 FLOPS = 2 * 512 * 512 * 512
 
 
@@ -71,9 +71,9 @@ def tile_attend_ghash_tnh_pl_kernel(tc, W, dz, eT, cd, offs, out_0, out_1, out_2
         w_scales = tile("w_scales", [P, FEATURES], U8)
         w_dealt = w_raw[:].rearrange("p j (m t) -> p m j t", t=LANES)
         w_bf = [tile("w_bf%d" % h, [P, 2, P, LANES], BF16) for h in range(2)]
-        for h, engine_copy in enumerate((nc.vector.tensor_copy, nc.scalar.copy)):
+        for h, engine_copy in enumerate((nc.scalar.copy, nc.vector.tensor_copy)):
             engine_copy(out=w_bf[h][:].rearrange("p t m j -> p m j t"), in_=w_dealt[:, :, :, 2 * h : 2 * h + 2])
-        for h in range(2):
+        for h in (1, 0):
             span = slice(2 * h * P, 2 * (h + 1) * P)
             nc.vector.quantize_mx(
                 out=w_codes[:, span].bitcast(E4M3),
@@ -82,7 +82,7 @@ def tile_attend_ghash_tnh_pl_kernel(tc, W, dz, eT, cd, offs, out_0, out_1, out_2
             )
 
         sums = [psum.tile([P, ITEMS], F32, name="sums%d" % t) for t in range(LANES)]
-        for t in (0, 1, 3, 2):
+        for t in (2, 3, 1, 0):
             nc.tensor.matmul_mx(
                 out=sums[t][:],
                 lhsT=w_codes[:, t * P : (t + 1) * P].bitcast(E4M3),
@@ -93,31 +93,34 @@ def tile_attend_ghash_tnh_pl_kernel(tc, W, dz, eT, cd, offs, out_0, out_1, out_2
                 stop=True,
             )
 
-        scaled = {t: tile("scaled%d" % t, [P, ITEMS], F32) for t in (0, 1, 3)}
+        scaled = {t: tile("scaled%d" % t, [P, ITEMS], F32) for t in (2, 3)}
         slope = [tile("slope%d" % t, [P, ITEMS], F32) for t in range(LANES)]
 
         sig = tile("sig0", [P, ITEMS], F32, "clear2")
-        nc.scalar.activation(out=sig[:], in_=table[0][:].indirect(offsets[:]), func=ACT.Sigmoid, scale=2.0)
-        nc.vector.tensor_scalar(scaled[0][:], sums[0][:], weights[:, 0:1], -4.0, ALU.mult, ALU.mult)
-        for t in (1, 3):
-            nc.vector.tensor_scalar(scaled[t][:], sums[t][:], weights[:, t : t + 1], None, ALU.mult)
-        nc.vector.scalar_tensor_tensor(slope[0][:], sig[:], 1.0, sig[:], ALU.subtract, ALU.mult)
+        nc.scalar.activation(out=sig[:], in_=table[2][:].indirect(offsets[:]), func=ACT.Sigmoid, scale=2.0)
+        nc.vector.tensor_scalar(scaled[2][:], sums[2][:], weights[:, 2:3], -4.0, ALU.mult, ALU.mult)
+        nc.vector.tensor_scalar(scaled[3][:], sums[3][:], weights[:, 3:4], None, ALU.mult)
+        scaled[1] = tile("scaled1", [P, ITEMS], F32, "table2")
+        nc.scalar.activation(out=scaled[1][:], in_=sums[1][:], func=ACT.Copy, scale=weights[:, 1:2])
+        nc.vector.scalar_tensor_tensor(slope[2][:], sig[:], 1.0, sig[:], ALU.subtract, ALU.mult)
 
         for turn in (2, 3):
             t = ORDER[turn]
             result[t] = tile("result%d" % t, [P, COLUMNS], F32, "clear%d" % turn)
             nc.gpsimd.memset(result[t][:], 0.0)
 
-        front_pairs = [tile("front_pairs%d" % c, [P, 2, CHUNK, 2], BF16) for c in range(2)]
+        front_pairs = tile("front_pairs", [P, 2, 2, CHUNK, 2], BF16)
 
         def unit_tile(name, tag):
             unit = tile(name, [P, 1], F32, tag)
             nc.gpsimd.memset(unit[:], 1.0)
             return unit
 
-        def pool_round(c, t, unit):
-            source = result[t][:, c * CHUNK : (c + 1) * CHUNK]
-            nc.gpsimd.tensor_scalar(front_pairs[c][:, t // 2, :, t % 2], source, unit[:], -0.0, ALU.mult, ALU.add)
+        def pool_round(t, first, last, unit):
+            source = result[t][:, first * CHUNK : last * CHUNK].rearrange("p (g c) -> p g c", c=CHUNK)
+            nc.gpsimd.tensor_scalar(
+                front_pairs[:, first:last, t // 2, :, t % 2], source, unit[:], -0.0, ALU.mult, ALU.add
+            )
 
         for turn, t in enumerate(ORDER):
             if turn > 0:
@@ -129,7 +132,7 @@ def tile_attend_ghash_tnh_pl_kernel(tc, W, dz, eT, cd, offs, out_0, out_1, out_2
             if turn == 0:
                 nc.vector.tensor_tensor(result[t][:].indirect(offsets[:]), scaled[t][:], slope[t][:], ALU.mult)
             else:
-                grad = tile("grad%d" % t, [P, ITEMS], F32, {1: "grad2", 2: "grad1", 3: "slope1"}[turn])
+                grad = tile("grad%d" % t, [P, ITEMS], F32, {1: "grad0", 2: "grad1", 3: "slope1"}[turn])
                 if turn == 1:
                     nc.vector.scalar_tensor_tensor(
                         grad[:], sums[t][:], weights[:, t : t + 1], slope[t][:], ALU.mult, ALU.mult
@@ -139,16 +142,12 @@ def tile_attend_ghash_tnh_pl_kernel(tc, W, dz, eT, cd, offs, out_0, out_1, out_2
                 nc.vector.tensor_copy(result[t][:].indirect(offsets[:]), grad[:])
             nc.sync.dma_start(out=out_rows[:, t, :], in_=result[t][:])
             if turn == 0:
-                unit = unit_tile("unit0", "grad1")
-                for c in range(2):
-                    pool_round(c, 0, unit)
+                pool_round(2, 0, 2, unit_tile("unit0", "grad1"))
             if turn == 2:
-                pool_round(0, 2, unit_tile("unit1", "slope1"))
+                pool_round(0, 0, 1, unit_tile("unit1", "slope1"))
         unit = unit_tile("unit2", "slope3")
-        pool_round(1, 2, unit)
-        for c in range(2):
-            pool_round(c, 1, unit)
-        last_unit = unit_tile("unit3", "slope3")
+        pool_round(0, 1, 2, unit)
+        pool_round(1, 0, 2, unit)
 
         woven = [tile("woven%d" % c, [P, CHUNK, LANES], BF16) for c in range(4)]
         codes = tile("codes", [P, COLUMNS], U32)
@@ -162,7 +161,7 @@ def tile_attend_ghash_tnh_pl_kernel(tc, W, dz, eT, cd, offs, out_0, out_1, out_2
             nc.scalar.copy(out=back_pairs[c - 2][:, t // 2, :, t % 2], in_=result[t][:, c * CHUNK : (c + 1) * CHUNK])
 
         def weave_pairs(engine_copy, dtype, pairs, start, c, first, last):
-            words_in = pairs[:].rearrange("p u c e -> p u (c e)").bitcast(dtype)
+            words_in = pairs.rearrange("p u c e -> p u (c e)").bitcast(dtype)
             words = woven[c][:].rearrange("p c t -> p (c t)").bitcast(dtype).rearrange("p (c u) -> p c u", u=2)
             engine_copy(
                 out=words[:, first:last, :],
@@ -183,14 +182,12 @@ def tile_attend_ghash_tnh_pl_kernel(tc, W, dz, eT, cd, offs, out_0, out_1, out_2
             for c in (2, 3):
                 pair_up(c, t)
         for c in range(2):
-            nc.vector.tensor_scalar(
-                front_pairs[c][:, 1, :, 1], result[3][:, c * CHUNK : (c + 1) * CHUNK], last_unit[:], None, ALU.mult
-            )
+            nc.vector.tensor_copy(out=front_pairs[:, c, 1, :, 1], in_=result[3][:, c * CHUNK : (c + 1) * CHUNK])
         pair_up(2, 3)
-        weave_pairs(nc.scalar.copy, F32, back_pairs[0], 0, 2, 0, CHUNK)
+        weave_pairs(nc.scalar.copy, F32, back_pairs[0][:], 0, 2, 0, CHUNK)
         pair_up(3, 3)
         for c in range(2):
-            weave_pairs(nc.vector.tensor_copy, I32, front_pairs[c], 0, c, 0, CHUNK)
+            weave_pairs(nc.vector.tensor_copy, I32, front_pairs[:, c], 0, c, 0, CHUNK)
         quantise(0, 0, CHUNK // 2)
         quantise(0, CHUNK // 2, CHUNK)
         store_words(nc.sync, 0, CHUNK)
@@ -200,11 +197,12 @@ def tile_attend_ghash_tnh_pl_kernel(tc, W, dz, eT, cd, offs, out_0, out_1, out_2
         quantise(2, 0, CHUNK // 2)
         quantise(2, CHUNK // 2, CHUNK)
         store_words(nc.sync, 2 * CHUNK, 3 * CHUNK)
-        weave_pairs(nc.scalar.copy, F32, back_pairs[1], 0, 3, 0, CHUNK // 2)
+        weave_pairs(nc.scalar.copy, F32, back_pairs[1][:], 0, 3, 0, CHUNK // 2)
         quantise(3, 0, CHUNK // 2)
         store_words(nc.sync, 3 * CHUNK, 3 * CHUNK + CHUNK // 2)
-        weave_pairs(nc.scalar.copy, F32, back_pairs[1], 0, 3, CHUNK // 2, CHUNK)
-        quantise(3, CHUNK // 2, CHUNK)
+        for first in (CHUNK // 2, 3 * CHUNK // 4):
+            weave_pairs(nc.scalar.copy, F32, back_pairs[1][:], 0, 3, first, first + CHUNK // 4)
+            quantise(3, first, first + CHUNK // 4)
         store_words(nc.scalar, 3 * CHUNK + CHUNK // 2, COLUMNS)
         for q in range(4):
             queue = nc.sync if q % 2 == 0 else nc.scalar

@@ -19,6 +19,11 @@ ITEMS = 512
 FEATURES = 512
 COLUMNS = 2048
 CHUNK = 512
+HALF = 256
+LINK = 32
+FRONT = 1024
+EARLY = 640
+MIDDLE = 256
 ORDER = (2, 0, 1, 3)
 FLOPS = 2 * 512 * 512 * 512
 
@@ -53,19 +58,28 @@ def tile_attend_ghash_tnh_pl_kernel(tc, W, dz, eT, cd, offs, out_0, out_1, out_2
         nc.scalar.activation(out=warm[:], in_=weights[:, 0:1], func=ACT.Sigmoid)
         one = tile("one", [P, 1], F32, "pairs")
         nc.vector.memset(one[:], 1.0)
+        minus_half = tile("minus_half", [P, 1], F32)
+        nc.vector.memset(minus_half[:], -0.5)
         for t in ORDER[:2]:
             nc.vector.memset(result[t][:].bitcast(I32), 0)
+        result[ORDER[2]] = tile("result%d" % ORDER[2], [P, COLUMNS], F32)
+        nc.gpsimd.memset(result[ORDER[2]][:], 0.0)
 
-        dz_bf = tile("dz_bf", [P, ITEMS, LANES], BF16)
-        dz_codes = tile("dz_codes", [P, ITEMS], U32, "clear3")
+        dz_bf = [tile("dz_bf%d" % h, [P, HALF, LANES], BF16) for h in range(2)]
+        dz_codes = tile("dz_codes", [P, ITEMS], U32)
         dz_scales = tile("dz_scales", [P, ITEMS], U8)
-        nc.vector.tensor_copy(
-            out=dz_bf[:].rearrange("p (c i) j -> p c j i", i=4),
-            in_=dz_raw[:].rearrange("p j (c i) -> p c j i", i=4),
-        )
-        nc.vector.quantize_mx(
-            out=dz_codes[:].bitcast(E5M2), scales=dz_scales[:], in_=dz_bf[:].rearrange("p i j -> p (i j)")
-        )
+        for h, engine_copy in enumerate((nc.vector.tensor_copy, nc.scalar.copy)):
+            engine_copy(
+                out=dz_bf[h][:].rearrange("p (c i) j -> p c j i", i=4),
+                in_=dz_raw[:, :, h * HALF : (h + 1) * HALF].rearrange("p j (c i) -> p c j i", i=4),
+            )
+        for h in range(2):
+            span = slice(h * HALF, (h + 1) * HALF)
+            nc.vector.quantize_mx(
+                out=dz_codes[:, span].bitcast(E5M2),
+                scales=dz_scales[:, span],
+                in_=dz_bf[h][:].rearrange("p i j -> p (i j)"),
+            )
 
         w_codes = tile("w_codes", [P, FEATURES], U32)
         w_scales = tile("w_scales", [P, FEATURES], U8)
@@ -82,7 +96,7 @@ def tile_attend_ghash_tnh_pl_kernel(tc, W, dz, eT, cd, offs, out_0, out_1, out_2
             )
 
         sums = [psum.tile([P, ITEMS], F32, name="sums%d" % t) for t in range(LANES)]
-        for t in (2, 3, 1, 0):
+        for t in ORDER:
             nc.tensor.matmul_mx(
                 out=sums[t][:],
                 lhsT=w_codes[:, t * P : (t + 1) * P].bitcast(E4M3),
@@ -93,61 +107,74 @@ def tile_attend_ghash_tnh_pl_kernel(tc, W, dz, eT, cd, offs, out_0, out_1, out_2
                 stop=True,
             )
 
-        scaled = {t: tile("scaled%d" % t, [P, ITEMS], F32) for t in (2, 3)}
-        slope = [tile("slope%d" % t, [P, ITEMS], F32) for t in range(LANES)]
+        result[ORDER[3]] = tile("result%d" % ORDER[3], [P, COLUMNS], F32, "w_bf0")
+        nc.gpsimd.memset(result[ORDER[3]][:], 0.0)
 
-        sig = tile("sig0", [P, ITEMS], F32, "clear2")
-        nc.scalar.activation(out=sig[:], in_=table[2][:].indirect(offsets[:]), func=ACT.Sigmoid, scale=2.0)
-        nc.vector.tensor_scalar(scaled[2][:], sums[2][:], weights[:, 2:3], -4.0, ALU.mult, ALU.mult)
-        nc.vector.tensor_scalar(scaled[3][:], sums[3][:], weights[:, 3:4], None, ALU.mult)
-        scaled[1] = tile("scaled1", [P, ITEMS], F32, "table2")
-        nc.scalar.activation(out=scaled[1][:], in_=sums[1][:], func=ACT.Copy, scale=weights[:, 1:2])
-        nc.vector.scalar_tensor_tensor(slope[2][:], sig[:], 1.0, sig[:], ALU.subtract, ALU.mult)
+        scaled = {t: tile("scaled%d" % t, [P, ITEMS], F32) for t in ORDER}
+        first = ORDER[0]
+        nc.vector.tensor_scalar(scaled[first][:], sums[first][:], weights[:, first : first + 1], -4.0, ALU.mult, ALU.mult)
+        for t in ORDER[1:]:
+            nc.vector.tensor_scalar(scaled[t][:], sums[t][:], weights[:, t : t + 1], None, ALU.mult)
 
-        for turn in (2, 3):
-            t = ORDER[turn]
-            result[t] = tile("result%d" % t, [P, COLUMNS], F32, "clear%d" % turn)
-            nc.gpsimd.memset(result[t][:], 0.0)
-
-        front_pairs = tile("front_pairs", [P, 2, 2, CHUNK, 2], BF16)
+        front_pairs = tile("front_pairs", [P, 2, FRONT, 2], BF16)
 
         def unit_tile(name, tag):
             unit = tile(name, [P, 1], F32, tag)
             nc.gpsimd.memset(unit[:], 1.0)
             return unit
 
-        def pool_round(t, first, last, unit):
-            source = result[t][:, first * CHUNK : last * CHUNK].rearrange("p (g c) -> p g c", c=CHUNK)
+        def pool_round(t, columns, unit):
             nc.gpsimd.tensor_scalar(
-                front_pairs[:, first:last, t // 2, :, t % 2], source, unit[:], -0.0, ALU.mult, ALU.add
+                front_pairs[:, t // 2, columns, t % 2], result[t][:, columns], unit[:], -0.0, ALU.mult, ALU.add
             )
 
+        def window(t, items):
+            return result[t][:].indirect(offsets[:, items.start // 16 : items.stop // 16])
+
+        halves = (slice(0, HALF), slice(HALF, ITEMS))
+        whole = slice(0, ITEMS)
+        grads = {}
         for turn, t in enumerate(ORDER):
-            if turn > 0:
-                sig = tile("sig%d" % t, [P, ITEMS], F32, "turn%d" % turn)
-                tanh2 = tile("tanh2_%d" % t, [P, ITEMS], F32, "turn%d" % (turn + 1))
-                nc.scalar.activation(out=sig[:], in_=table[t][:].indirect(offsets[:]), func=ACT.Sigmoid, scale=2.0)
-                nc.scalar.activation(out=tanh2[:], in_=sig[:], func=ACT.Square, scale=2.0, bias=-1.0)
-                nc.scalar.activation(out=slope[t][:], in_=tanh2[:], func=ACT.Identity, scale=-1.0, bias=one[:])
+            sig = tile("sig%d" % t, [P, ITEMS], F32, "turn%d" % turn if turn > 0 else "sig_first")
+            slope = tile("slope%d" % t, [P, ITEMS], F32, "slope%d" % turn)
+            grad = tile("grad%d" % t, [P, ITEMS], F32, "slope%d" % (turn - 1) if turn > 1 else "grad%d" % turn)
+            grads[turn] = grad
+            nc.scalar.activation(out=sig[:], in_=table[t][:].indirect(offsets[:]), func=ACT.Sigmoid, scale=2.0)
             if turn == 0:
-                nc.vector.tensor_tensor(result[t][:].indirect(offsets[:]), scaled[t][:], slope[t][:], ALU.mult)
+                early, late = halves
+                square = tile("square", [P, ITEMS], F32)
+                own, shared = slice(0, HALF - LINK), slice(HALF - LINK, HALF)
+                squared = slice(shared.start, ITEMS)
+                nc.scalar.activation(out=square[:, squared], in_=sig[:, squared], func=ACT.Square, bias=minus_half[:])
+                nc.vector.scalar_tensor_tensor(slope[:, own], sig[:, own], 1.0, sig[:, own], ALU.subtract, ALU.mult)
+                nc.vector.tensor_scalar(slope[:, shared], square[:, shared], 0.25, None, ALU.subtract)
+                nc.vector.scalar_tensor_tensor(
+                    grad[:, late], square[:, late], 0.25, scaled[t][:, late], ALU.subtract, ALU.mult
+                )
+                nc.vector.tensor_tensor(window(t, early), scaled[t][:, early], slope[:, early], ALU.mult)
+                nc.vector.tensor_copy(window(t, late), grad[:, late])
             else:
-                grad = tile("grad%d" % t, [P, ITEMS], F32, {1: "grad0", 2: "grad1", 3: "slope1"}[turn])
-                if turn == 1:
-                    nc.vector.scalar_tensor_tensor(
-                        grad[:], sums[t][:], weights[:, t : t + 1], slope[t][:], ALU.mult, ALU.mult
+                tanh2 = tile("tanh2_%d" % t, [P, ITEMS], F32, "turn%d" % (turn + 1))
+                pieces = halves if turn == 1 else (whole,)
+                for items in pieces:
+                    nc.scalar.activation(out=tanh2[:, items], in_=sig[:, items], func=ACT.Square, scale=2.0, bias=-1.0)
+                for items in pieces:
+                    nc.scalar.activation(
+                        out=slope[:, items], in_=tanh2[:, items], func=ACT.Identity, scale=-1.0, bias=one[:]
                     )
-                else:
-                    nc.gpsimd.tensor_tensor(grad[:], scaled[t][:], slope[t][:], ALU.mult)
-                nc.vector.tensor_copy(result[t][:].indirect(offsets[:]), grad[:])
+                for items in pieces:
+                    nc.gpsimd.tensor_tensor(grad[:, items], scaled[t][:, items], slope[:, items], ALU.mult)
+                nc.vector.tensor_copy(window(t, whole), grad[:])
             nc.sync.dma_start(out=out_rows[:, t, :], in_=result[t][:])
-            if turn == 0:
-                pool_round(2, 0, 2, unit_tile("unit0", "grad1"))
+            if turn == 1:
+                pool_round(2, slice(0, EARLY), unit_tile("unit0", "slope1"))
             if turn == 2:
-                pool_round(0, 0, 1, unit_tile("unit1", "slope1"))
+                unit = unit_tile("unit1", "slope2")
+                pool_round(2, slice(EARLY, FRONT), unit)
+                pool_round(0, slice(0, MIDDLE), unit)
         unit = unit_tile("unit2", "slope3")
-        pool_round(0, 1, 2, unit)
-        pool_round(1, 0, 2, unit)
+        pool_round(0, slice(MIDDLE, FRONT), unit)
+        pool_round(1, slice(0, FRONT), unit)
 
         woven = [tile("woven%d" % c, [P, CHUNK, LANES], BF16) for c in range(4)]
         codes = tile("codes", [P, COLUMNS], U32)
@@ -182,12 +209,13 @@ def tile_attend_ghash_tnh_pl_kernel(tc, W, dz, eT, cd, offs, out_0, out_1, out_2
             for c in (2, 3):
                 pair_up(c, t)
         for c in range(2):
-            nc.vector.tensor_copy(out=front_pairs[:, c, 1, :, 1], in_=result[3][:, c * CHUNK : (c + 1) * CHUNK])
+            span = slice(c * CHUNK, (c + 1) * CHUNK)
+            nc.vector.tensor_copy(out=front_pairs[:, 1, span, 1], in_=result[3][:, span])
         pair_up(2, 3)
         weave_pairs(nc.scalar.copy, F32, back_pairs[0][:], 0, 2, 0, CHUNK)
         pair_up(3, 3)
         for c in range(2):
-            weave_pairs(nc.vector.tensor_copy, I32, front_pairs[:, c], 0, c, 0, CHUNK)
+            weave_pairs(nc.vector.tensor_copy, I32, front_pairs[:], c * CHUNK, c, 0, CHUNK)
         quantise(0, 0, CHUNK // 2)
         quantise(0, CHUNK // 2, CHUNK)
         store_words(nc.sync, 0, CHUNK)

@@ -20,12 +20,10 @@ FEATURES = 512
 COLUMNS = 2048
 CHUNK = 512
 HALF = 256
-LINK = 32
-FRONT = 1024
-EARLY = 640
-MIDDLE = 256
-ORDER = (2, 0, 1, 3)
+SPARE = 8
 FLOPS = 2 * 512 * 512 * 512
+A, B, C, D = 2, 3, 0, 1
+GAP = 256
 
 
 def tile_attend_ghash_tnh_pl_kernel(tc, W, dz, eT, cd, offs, out_0, out_1, out_2):
@@ -42,7 +40,8 @@ def tile_attend_ghash_tnh_pl_kernel(tc, W, dz, eT, cd, offs, out_0, out_1, out_2
         dz_raw = tile("dz_raw", [P, LANES, ITEMS], F32)
         w_raw = tile("w_raw", [P, LANES, FEATURES], F32)
         table = [tile("table%d" % t, [P, COLUMNS], F32) for t in range(LANES)]
-        result = {t: tile("result%d" % t, [P, COLUMNS], F32) for t in ORDER[:2]}
+        result = {t: tile("result%d" % t, [P, COLUMNS], F32) for t in (A, B)}
+        result[C] = tile("result%d" % C, [P, COLUMNS + SPARE], F32)
 
         eT_rows = eT.rearrange("(p t) c -> p t c", t=LANES)
         out_rows = out_0.rearrange("(p t) c -> p t c", t=LANES)
@@ -51,19 +50,20 @@ def tile_attend_ghash_tnh_pl_kernel(tc, W, dz, eT, cd, offs, out_0, out_1, out_2
         nc.sync.dma_start(out=w_raw[:], in_=W.rearrange("(p j) d -> p j d", j=LANES))
         nc.sync.dma_start(offsets[:], offs)
         nc.scalar.dma_start(out=weights[:], in_=cd.rearrange("(p t) o -> p (t o)", t=LANES))
-        for t in ORDER:
+        for t in (A, B, C, D):
             nc.sync.dma_start(out=table[t][:], in_=eT_rows[:, t, :])
 
         warm = tile("warm", [P, 1], F32)
         nc.scalar.activation(out=warm[:], in_=weights[:, 0:1], func=ACT.Sigmoid)
-        one = tile("one", [P, 1], F32, "pairs")
-        nc.vector.memset(one[:], 1.0)
-        minus_half = tile("minus_half", [P, 1], F32)
-        nc.vector.memset(minus_half[:], -0.5)
-        for t in ORDER[:2]:
+        for t in (A, B):
             nc.vector.memset(result[t][:].bitcast(I32), 0)
-        result[ORDER[2]] = tile("result%d" % ORDER[2], [P, COLUMNS], F32)
-        nc.gpsimd.memset(result[ORDER[2]][:], 0.0)
+        nc.gpsimd.memset(result[C][:, :COLUMNS], 0.0)
+        nc.gpsimd.memset(result[C][:, COLUMNS:], 1.0)
+        one = result[C][:, COLUMNS : COLUMNS + 1]
+        factors = tile("factors", [P, 2], F32)
+        nc.vector.tensor_scalar(factors[:, 0:1], weights[:, D : D + 1], -1.0, None, ALU.mult)
+        unit_c = tile("unit_c", [P, 1], F32)
+        nc.vector.memset(unit_c[:], 1.0)
 
         dz_bf = [tile("dz_bf%d" % h, [P, HALF, LANES], BF16) for h in range(2)]
         dz_codes = tile("dz_codes", [P, ITEMS], U32)
@@ -96,7 +96,7 @@ def tile_attend_ghash_tnh_pl_kernel(tc, W, dz, eT, cd, offs, out_0, out_1, out_2
             )
 
         sums = [psum.tile([P, ITEMS], F32, name="sums%d" % t) for t in range(LANES)]
-        for t in ORDER:
+        for t in (A, B, C, D):
             nc.tensor.matmul_mx(
                 out=sums[t][:],
                 lhsT=w_codes[:, t * P : (t + 1) * P].bitcast(E4M3),
@@ -107,74 +107,121 @@ def tile_attend_ghash_tnh_pl_kernel(tc, W, dz, eT, cd, offs, out_0, out_1, out_2
                 stop=True,
             )
 
-        result[ORDER[3]] = tile("result%d" % ORDER[3], [P, COLUMNS], F32, "w_bf0")
-        nc.gpsimd.memset(result[ORDER[3]][:], 0.0)
+        result[D] = tile("result%d" % D, [P, COLUMNS], F32, "w_bf0")
+        nc.gpsimd.memset(result[D][:], 0.0)
 
-        scaled = {t: tile("scaled%d" % t, [P, ITEMS], F32) for t in ORDER}
-        first = ORDER[0]
-        nc.vector.tensor_scalar(scaled[first][:], sums[first][:], weights[:, first : first + 1], -4.0, ALU.mult, ALU.mult)
-        for t in ORDER[1:]:
-            nc.vector.tensor_scalar(scaled[t][:], sums[t][:], weights[:, t : t + 1], None, ALU.mult)
+        halves = (slice(0, HALF), slice(HALF, ITEMS))
 
-        front_pairs = tile("front_pairs", [P, 2, FRONT, 2], BF16)
+        def scale_out(out, t, items):
+            nc.vector.tensor_scalar(out, sums[t][:, items], weights[:, t : t + 1], None, ALU.mult)
+
+        def gather(t):
+            sig = tile("sig%d" % t, [P, ITEMS], F32)
+            nc.scalar.activation(out=sig[:], in_=table[t][:].indirect(offsets[:]), func=ACT.Sigmoid, scale=2.0)
+            return sig
+
+        def square(out, sig, bias):
+            nc.scalar.activation(out=out, in_=sig, func=ACT.Square, scale=-2.0, bias=bias)
+
+        def store_plane(t):
+            nc.sync.dma_start(out=out_rows[:, t, :], in_=result[t][:, :COLUMNS])
+
+        pairs = [tile("pairs%d" % c, [P, 2, CHUNK + SPARE, 2], BF16) for c in range(4)]
+
+        def spot(t, c, first=0, last=CHUNK):
+            return pairs[c][:, t // 2, first:last, t % 2], result[t][:, c * CHUNK + first : c * CHUNK + last]
 
         def unit_tile(name, tag):
             unit = tile(name, [P, 1], F32, tag)
             nc.gpsimd.memset(unit[:], 1.0)
             return unit
 
-        def pool_round(t, columns, unit):
-            nc.gpsimd.tensor_scalar(
-                front_pairs[:, t // 2, columns, t % 2], result[t][:, columns], unit[:], -0.0, ALU.mult, ALU.add
-            )
+        def pool_round(t, c, unit, first=0, last=CHUNK):
+            out, source = spot(t, c, first, last)
+            nc.gpsimd.tensor_scalar(out, source, unit[:], -0.0, ALU.mult, ALU.add)
 
-        def window(t, items):
-            return result[t][:].indirect(offsets[:, items.start // 16 : items.stop // 16])
-
-        halves = (slice(0, HALF), slice(HALF, ITEMS))
         whole = slice(0, ITEMS)
-        grads = {}
-        for turn, t in enumerate(ORDER):
-            sig = tile("sig%d" % t, [P, ITEMS], F32, "turn%d" % turn if turn > 0 else "sig_first")
-            slope = tile("slope%d" % t, [P, ITEMS], F32, "slope%d" % turn)
-            grad = tile("grad%d" % t, [P, ITEMS], F32, "slope%d" % (turn - 1) if turn > 1 else "grad%d" % turn)
-            grads[turn] = grad
-            nc.scalar.activation(out=sig[:], in_=table[t][:].indirect(offsets[:]), func=ACT.Sigmoid, scale=2.0)
-            if turn == 0:
-                early, late = halves
-                square = tile("square", [P, ITEMS], F32)
-                own, shared = slice(0, HALF - LINK), slice(HALF - LINK, HALF)
-                squared = slice(shared.start, ITEMS)
-                nc.scalar.activation(out=square[:, squared], in_=sig[:, squared], func=ACT.Square, bias=minus_half[:])
-                nc.vector.scalar_tensor_tensor(slope[:, own], sig[:, own], 1.0, sig[:, own], ALU.subtract, ALU.mult)
-                nc.vector.tensor_scalar(slope[:, shared], square[:, shared], 0.25, None, ALU.subtract)
-                nc.vector.scalar_tensor_tensor(
-                    grad[:, late], square[:, late], 0.25, scaled[t][:, late], ALU.subtract, ALU.mult
-                )
-                nc.vector.tensor_tensor(window(t, early), scaled[t][:, early], slope[:, early], ALU.mult)
-                nc.vector.tensor_copy(window(t, late), grad[:, late])
-            else:
-                tanh2 = tile("tanh2_%d" % t, [P, ITEMS], F32, "turn%d" % (turn + 1))
-                pieces = halves if turn == 1 else (whole,)
-                for items in pieces:
-                    nc.scalar.activation(out=tanh2[:, items], in_=sig[:, items], func=ACT.Square, scale=2.0, bias=-1.0)
-                for items in pieces:
-                    nc.scalar.activation(
-                        out=slope[:, items], in_=tanh2[:, items], func=ACT.Identity, scale=-1.0, bias=one[:]
-                    )
-                for items in pieces:
-                    nc.gpsimd.tensor_tensor(grad[:, items], scaled[t][:, items], slope[:, items], ALU.mult)
-                nc.vector.tensor_copy(window(t, whole), grad[:])
-            nc.sync.dma_start(out=out_rows[:, t, :], in_=result[t][:])
-            if turn == 1:
-                pool_round(2, slice(0, EARLY), unit_tile("unit0", "slope1"))
-            if turn == 2:
-                unit = unit_tile("unit1", "slope2")
-                pool_round(2, slice(EARLY, FRONT), unit)
-                pool_round(0, slice(0, MIDDLE), unit)
-        unit = unit_tile("unit2", "slope3")
-        pool_round(0, slice(MIDDLE, FRONT), unit)
-        pool_round(1, slice(0, FRONT), unit)
+        scaled = {t: tile("scaled%d" % t, [P, ITEMS], F32) for t in (A, B)}
+        nc.vector.tensor_scalar(scaled[A][:], sums[A][:], weights[:, A : A + 1], -1.0, ALU.mult, ALU.mult)
+        scale_out(scaled[B][:], B, whole)
+        scaled_c = [tile("scaled_c0", [P, HALF], F32)]
+        scale_out(scaled_c[0][:], C, halves[0])
+
+        sig = gather(A)
+        grad = tile("grad_a", [P, ITEMS], F32)
+        squares = [tile("square_a%d" % h, [P, HALF], F32) for h in range(2)]
+        for h, items in enumerate(halves):
+            square(squares[h][:], sig[:, items], unit_c[:])
+        for h, items in enumerate(halves):
+            nc.vector.scalar_tensor_tensor(grad[:, items], squares[h][:], 1.0, scaled[A][:, items], ALU.subtract, ALU.mult)
+        scaled_c.append(tile("scaled_c1", [P, HALF], F32, "square_a0"))
+        scale_out(scaled_c[1][:], C, halves[1])
+        nc.vector.tensor_copy(result[A][:].indirect(offsets[:]), grad[:])
+        store_plane(A)
+
+        sig = gather(B)
+        tanh2 = tile("tanh2_b", [P, ITEMS], F32)
+        slope = tile("slope_b", [P, ITEMS], F32)
+        grad = tile("grad_b", [P, ITEMS], F32)
+        for items in halves:
+            square(tanh2[:, items], sig[:, items], unit_c[:])
+        for items in halves:
+            nc.gpsimd.tensor_scalar(slope[:, items], tanh2[:, items], -1.0, 1.0, ALU.mult, ALU.add)
+        for items in halves:
+            nc.gpsimd.tensor_tensor(grad[:, items], scaled[B][:, items], slope[:, items], ALU.mult)
+        nc.vector.tensor_copy(result[B][:].indirect(offsets[:]), grad[:])
+        store_plane(B)
+        pool_round(A, 1, unit_tile("unit0", "slope_b"))
+
+        sig = gather(C)
+        tanh2 = tile("tanh2_c", [P, ITEMS], F32)
+        slope = tile("slope_c", [P, ITEMS], F32)
+        grad_c = tile("grad_c", [P, ITEMS], F32)
+        for items in halves:
+            square(tanh2[:, items], sig[:, items], unit_c[:])
+        for items in halves:
+            nc.scalar.activation(out=slope[:, items], in_=tanh2[:, items], func=ACT.Identity, scale=-1.0, bias=unit_c[:])
+        for h, items in enumerate(halves):
+            nc.gpsimd.tensor_tensor(grad_c[:, items], scaled_c[h][:], slope[:, items], ALU.mult)
+        pool_round(A, 0, unit_tile("unit1", "slope_c"), 0, GAP)
+
+        sig = gather(D)
+        tanh2 = tile("tanh2_d", [P, ITEMS], F32)
+        slope = tile("slope_d", [P, ITEMS], F32)
+        grad = tile("grad_d", [P, ITEMS], F32)
+        square(tanh2[:, halves[0]], sig[:, halves[0]], one)
+        square(tanh2[:, halves[1]], sig[:, halves[1]], unit_c[:])
+        for items in halves:
+            nc.gpsimd.tensor_scalar(
+                slope[:, items], tanh2[:, items], factors[:, 0:1], weights[:, D : D + 1], ALU.mult, ALU.add
+            )
+        nc.scalar.activation(out=result[C][:].indirect(offsets[:]), in_=grad_c[:], func=ACT.Copy)
+        store_plane(C)
+        for items in halves:
+            nc.vector.tensor_tensor(grad[:, items], slope[:, items], sums[D][:, items], ALU.mult)
+        nc.vector.tensor_copy(result[D][:].indirect(offsets[:]), grad[:])
+        store_plane(D)
+
+        unit = unit_tile("unit2", "tanh2_d")
+        pool_round(A, 2, unit)
+        pool_round(A, 3, unit)
+        pool_round(A, 0, unit, GAP, CHUNK)
+        for c in (2, 3, 0):
+            pool_round(B, c, unit)
+
+        def scalar_round(t, c, last=CHUNK):
+            out, source = spot(t, c, 0, last)
+            nc.scalar.copy(out=out, in_=source)
+
+        scalar_round(C, 2)
+        scalar_round(C, 3, CHUNK + 1)
+        scalar_round(C, 0)
+        scalar_round(C, 1)
+        one_bf = pairs[3][:, C // 2, CHUNK : CHUNK + 1, C % 2]
+
+        def vector_round(t, c):
+            out, source = spot(t, c)
+            nc.vector.tensor_scalar(out, source, one_bf, None, ALU.mult)
 
         woven = [tile("woven%d" % c, [P, CHUNK, LANES], BF16) for c in range(4)]
         codes = tile("codes", [P, COLUMNS], U32)
@@ -182,18 +229,10 @@ def tile_attend_ghash_tnh_pl_kernel(tc, W, dz, eT, cd, offs, out_0, out_1, out_2
         words_out = out_1[0].rearrange("p c l -> p (c l)").bitcast(I32)
         scales_out = out_2[0].bitcast(I32).rearrange("r (a c) -> a r c", a=4)
 
-        back_pairs = [tile("pairs", [P, 2, CHUNK, 2], BF16), tile("pairs3", [P, 2, CHUNK, 2], BF16, "turn4")]
-
-        def pair_up(c, t):
-            nc.scalar.copy(out=back_pairs[c - 2][:, t // 2, :, t % 2], in_=result[t][:, c * CHUNK : (c + 1) * CHUNK])
-
-        def weave_pairs(engine_copy, dtype, pairs, start, c, first, last):
-            words_in = pairs.rearrange("p u c e -> p u (c e)").bitcast(dtype)
+        def weave(engine_copy, dtype, c, first, last):
+            words_in = pairs[c][:].rearrange("p u c e -> p u (c e)").bitcast(dtype)
             words = woven[c][:].rearrange("p c t -> p (c t)").bitcast(dtype).rearrange("p (c u) -> p c u", u=2)
-            engine_copy(
-                out=words[:, first:last, :],
-                in_=words_in[:, :, start + first : start + last].rearrange("p u c -> p c u"),
-            )
+            engine_copy(out=words[:, first:last, :], in_=words_in[:, :, first:last].rearrange("p u c -> p c u"))
 
         def quantise(c, first, last):
             nc.vector.quantize_mx(
@@ -205,33 +244,24 @@ def tile_attend_ghash_tnh_pl_kernel(tc, W, dz, eT, cd, offs, out_0, out_1, out_2
         def store_words(queue, first, last):
             queue.dma_start(out=words_out[:, first:last], in_=codes[:, first:last].bitcast(I32))
 
-        for t in ORDER[:3]:
-            for c in (2, 3):
-                pair_up(c, t)
-        for c in range(2):
-            span = slice(c * CHUNK, (c + 1) * CHUNK)
-            nc.vector.tensor_copy(out=front_pairs[:, 1, span, 1], in_=result[3][:, span])
-        pair_up(2, 3)
-        weave_pairs(nc.scalar.copy, F32, back_pairs[0][:], 0, 2, 0, CHUNK)
-        pair_up(3, 3)
-        for c in range(2):
-            weave_pairs(nc.vector.tensor_copy, I32, front_pairs[:], c * CHUNK, c, 0, CHUNK)
-        quantise(0, 0, CHUNK // 2)
-        quantise(0, CHUNK // 2, CHUNK)
-        store_words(nc.sync, 0, CHUNK)
-        quantise(1, 0, CHUNK // 2)
-        quantise(1, CHUNK // 2, CHUNK)
-        store_words(nc.sync, CHUNK, 2 * CHUNK)
-        quantise(2, 0, CHUNK // 2)
-        quantise(2, CHUNK // 2, CHUNK)
+        vector_round(D, 2)
+        vector_round(D, 3)
+        scalar_round(D, 0)
+        scalar_round(D, 1)
+        weave(nc.vector.tensor_copy, I32, 2, 0, CHUNK)
+        weave(nc.vector.tensor_copy, I32, 3, 0, CHUNK)
+        vector_round(B, 1)
+        quantise(2, 0, CHUNK)
         store_words(nc.sync, 2 * CHUNK, 3 * CHUNK)
-        weave_pairs(nc.scalar.copy, F32, back_pairs[1][:], 0, 3, 0, CHUNK // 2)
-        quantise(3, 0, CHUNK // 2)
-        store_words(nc.sync, 3 * CHUNK, 3 * CHUNK + CHUNK // 2)
-        for first in (CHUNK // 2, 3 * CHUNK // 4):
-            weave_pairs(nc.scalar.copy, F32, back_pairs[1][:], 0, 3, first, first + CHUNK // 4)
-            quantise(3, first, first + CHUNK // 4)
-        store_words(nc.scalar, 3 * CHUNK + CHUNK // 2, COLUMNS)
+        weave(nc.vector.tensor_copy, I32, 0, 0, CHUNK)
+        quantise(3, 0, CHUNK)
+        store_words(nc.sync, 3 * CHUNK, 4 * CHUNK)
+        quantise(0, 0, CHUNK)
+        store_words(nc.sync, 0, CHUNK)
+        for first in (0, HALF):
+            weave(nc.scalar.copy, F32, 1, first, first + HALF)
+            quantise(1, first, first + HALF)
+        store_words(nc.scalar, CHUNK, 2 * CHUNK)
         for q in range(4):
             queue = nc.sync if q % 2 == 0 else nc.scalar
             queue.dma_start(out=scales_out[:, 4 * q : 4 * q + 4, :], in_=scales[32 * q : 32 * q + 16, :].bitcast(I32))

@@ -20,10 +20,11 @@ FEATURES = 512
 COLUMNS = 2048
 CHUNK = 512
 HALF = 256
+LINK = 32
 SPARE = 8
+ORDER = (2, 3, 0, 1)
+POOL_B = 320
 FLOPS = 2 * 512 * 512 * 512
-A, B, C, D = 2, 3, 0, 1
-GAP = 256
 
 
 def tile_attend_ghash_tnh_pl_kernel(tc, W, dz, eT, cd, offs, out_0, out_1, out_2):
@@ -40,8 +41,9 @@ def tile_attend_ghash_tnh_pl_kernel(tc, W, dz, eT, cd, offs, out_0, out_1, out_2
         dz_raw = tile("dz_raw", [P, LANES, ITEMS], F32)
         w_raw = tile("w_raw", [P, LANES, FEATURES], F32)
         table = [tile("table%d" % t, [P, COLUMNS], F32) for t in range(LANES)]
-        result = {t: tile("result%d" % t, [P, COLUMNS], F32) for t in (A, B)}
-        result[C] = tile("result%d" % C, [P, COLUMNS + SPARE], F32)
+        A, B, C, D = ORDER
+        result = {t: tile("result%d" % t, [P, COLUMNS + SPARE], F32) for t in (A, C)}
+        result[B] = tile("result%d" % B, [P, COLUMNS], F32)
 
         eT_rows = eT.rearrange("(p t) c -> p t c", t=LANES)
         out_rows = out_0.rearrange("(p t) c -> p t c", t=LANES)
@@ -50,20 +52,18 @@ def tile_attend_ghash_tnh_pl_kernel(tc, W, dz, eT, cd, offs, out_0, out_1, out_2
         nc.sync.dma_start(out=w_raw[:], in_=W.rearrange("(p j) d -> p j d", j=LANES))
         nc.sync.dma_start(offsets[:], offs)
         nc.scalar.dma_start(out=weights[:], in_=cd.rearrange("(p t) o -> p (t o)", t=LANES))
-        for t in (A, B, C, D):
+        for t in ORDER:
             nc.sync.dma_start(out=table[t][:], in_=eT_rows[:, t, :])
 
         warm = tile("warm", [P, 1], F32)
         nc.scalar.activation(out=warm[:], in_=weights[:, 0:1], func=ACT.Sigmoid)
-        for t in (A, B):
-            nc.vector.memset(result[t][:].bitcast(I32), 0)
+        minus_half = tile("minus_half", [P, 1], F32)
+        nc.vector.memset(minus_half[:], -0.5)
+        for t in ORDER[:2]:
+            nc.vector.memset(result[t][:, :COLUMNS].bitcast(I32), 0)
+        nc.vector.memset(result[A][:, COLUMNS:], 1.0)
         nc.gpsimd.memset(result[C][:, :COLUMNS], 0.0)
         nc.gpsimd.memset(result[C][:, COLUMNS:], 1.0)
-        one = result[C][:, COLUMNS : COLUMNS + 1]
-        factors = tile("factors", [P, 2], F32)
-        nc.vector.tensor_scalar(factors[:, 0:1], weights[:, D : D + 1], -1.0, None, ALU.mult)
-        unit_c = tile("unit_c", [P, 1], F32)
-        nc.vector.memset(unit_c[:], 1.0)
 
         dz_bf = [tile("dz_bf%d" % h, [P, HALF, LANES], BF16) for h in range(2)]
         dz_codes = tile("dz_codes", [P, ITEMS], U32)
@@ -96,7 +96,7 @@ def tile_attend_ghash_tnh_pl_kernel(tc, W, dz, eT, cd, offs, out_0, out_1, out_2
             )
 
         sums = [psum.tile([P, ITEMS], F32, name="sums%d" % t) for t in range(LANES)]
-        for t in (A, B, C, D):
+        for t in ORDER:
             nc.tensor.matmul_mx(
                 out=sums[t][:],
                 lhsT=w_codes[:, t * P : (t + 1) * P].bitcast(E4M3),
@@ -110,118 +110,104 @@ def tile_attend_ghash_tnh_pl_kernel(tc, W, dz, eT, cd, offs, out_0, out_1, out_2
         result[D] = tile("result%d" % D, [P, COLUMNS], F32, "w_bf0")
         nc.gpsimd.memset(result[D][:], 0.0)
 
+        whole = slice(0, ITEMS)
+        extra = slice(ITEMS, ITEMS + SPARE)
+        linked = slice(0, ITEMS + 1)
         halves = (slice(0, HALF), slice(HALF, ITEMS))
+        scaled = {t: tile("scaled%d" % t, [P, ITEMS + SPARE], F32) for t in ORDER}
+        factor = {A: -4.0, B: 1.0, C: 1.0, D: -1.0}
+        slopes = {t: tile("slope%d" % t, [P, ITEMS + SPARE], F32) for t in ORDER}
+        for t in (C, D):
+            nc.vector.memset(scaled[t][:, extra], factor[t])
+            nc.vector.memset(slopes[t][:, extra], 0.0 if t == D else 1.0)
+        for t in ORDER:
+            nc.vector.tensor_scalar(scaled[t][:, whole], sums[t][:], weights[:, t : t + 1], factor[t], ALU.mult, ALU.mult)
 
-        def scale_out(out, t, items):
-            nc.vector.tensor_scalar(out, sums[t][:, items], weights[:, t : t + 1], None, ALU.mult)
+        back = tile("back", [P, 4 * (2 * CHUNK + SPARE)], BF16)
+        front = [tile("front%d" % c, [P, 4 * CHUNK], BF16) for c in range(2)]
 
-        def gather(t):
-            sig = tile("sig%d" % t, [P, ITEMS], F32)
+        def home(first):
+            if first >= 2 * CHUNK:
+                return back, 2 * CHUNK
+            return front[first // CHUNK], first // CHUNK * CHUNK
+
+        def spot(t, first, last):
+            pairs, start = home(first)
+            base = t // 2 * (pairs.shape[1] // 2) + t % 2
+            return pairs[:, base + 2 * (first - start) : base + 2 * (last - start) - 1 : 2], result[t][:, first:last]
+
+        def pool_round(t, first, last, unit):
+            out, source = spot(t, first, last)
+            nc.gpsimd.tensor_scalar(out, source, unit, -0.0, ALU.mult, ALU.add)
+
+        def scalar_round(t, first, last):
+            out, source = spot(t, first, last)
+            nc.scalar.copy(out=out, in_=source)
+
+        def vector_round(t, first, last, unit, other):
+            out, source = spot(t, first, last)
+            nc.vector.tensor_scalar(out, source, unit, other, ALU.mult, ALU.mult)
+
+        def window(t, items):
+            return result[t][:].indirect(offsets[:, items.start // 16 : items.stop // 16])
+
+        def gather(t, tag):
+            sig = tile("sig%d" % t, [P, ITEMS], F32, tag)
             nc.scalar.activation(out=sig[:], in_=table[t][:].indirect(offsets[:]), func=ACT.Sigmoid, scale=2.0)
             return sig
-
-        def square(out, sig, bias):
-            nc.scalar.activation(out=out, in_=sig, func=ACT.Square, scale=-2.0, bias=bias)
 
         def store_plane(t):
             nc.sync.dma_start(out=out_rows[:, t, :], in_=result[t][:, :COLUMNS])
 
-        pairs = [tile("pairs%d" % c, [P, 2, CHUNK + SPARE, 2], BF16) for c in range(4)]
+        grads = {t: tile("grad%d" % t, [P, ITEMS + SPARE], F32) for t in ORDER}
+        units = {t: grads[t][:, ITEMS : ITEMS + 1] for t in ORDER}
 
-        def spot(t, c, first=0, last=CHUNK):
-            return pairs[c][:, t // 2, first:last, t % 2], result[t][:, c * CHUNK + first : c * CHUNK + last]
-
-        def unit_tile(name, tag):
-            unit = tile(name, [P, 1], F32, tag)
-            nc.gpsimd.memset(unit[:], 1.0)
-            return unit
-
-        def pool_round(t, c, unit, first=0, last=CHUNK):
-            out, source = spot(t, c, first, last)
-            nc.gpsimd.tensor_scalar(out, source, unit[:], -0.0, ALU.mult, ALU.add)
-
-        whole = slice(0, ITEMS)
-        scaled = {t: tile("scaled%d" % t, [P, ITEMS], F32) for t in (A, B)}
-        nc.vector.tensor_scalar(scaled[A][:], sums[A][:], weights[:, A : A + 1], -1.0, ALU.mult, ALU.mult)
-        scale_out(scaled[B][:], B, whole)
-        scaled_c = [tile("scaled_c0", [P, HALF], F32)]
-        scale_out(scaled_c[0][:], C, halves[0])
-
-        sig = gather(A)
-        grad = tile("grad_a", [P, ITEMS], F32)
-        squares = [tile("square_a%d" % h, [P, HALF], F32) for h in range(2)]
-        for h, items in enumerate(halves):
-            square(squares[h][:], sig[:, items], unit_c[:])
-        for h, items in enumerate(halves):
-            nc.vector.scalar_tensor_tensor(grad[:, items], squares[h][:], 1.0, scaled[A][:, items], ALU.subtract, ALU.mult)
-        scaled_c.append(tile("scaled_c1", [P, HALF], F32, "square_a0"))
-        scale_out(scaled_c[1][:], C, halves[1])
-        nc.vector.tensor_copy(result[A][:].indirect(offsets[:]), grad[:])
+        sig, slope, grad = gather(A, "sig_first"), slopes[A], grads[A]
+        early, late = halves
+        square = tile("square", [P, ITEMS], F32)
+        own, shared = slice(0, HALF - LINK), slice(HALF - LINK, HALF)
+        squared = slice(shared.start, ITEMS)
+        nc.scalar.activation(out=square[:, squared], in_=sig[:, squared], func=ACT.Square, bias=minus_half[:])
+        nc.vector.scalar_tensor_tensor(slope[:, own], sig[:, own], 1.0, sig[:, own], ALU.subtract, ALU.mult)
+        nc.vector.tensor_scalar(slope[:, shared], square[:, shared], 0.25, None, ALU.subtract)
+        nc.vector.scalar_tensor_tensor(grad[:, late], square[:, late], 0.25, scaled[A][:, late], ALU.subtract, ALU.mult)
+        nc.vector.tensor_tensor(window(A, early), scaled[A][:, early], slope[:, early], ALU.mult)
+        nc.vector.tensor_copy(window(A, late), grad[:, late])
         store_plane(A)
 
-        sig = gather(B)
-        tanh2 = tile("tanh2_b", [P, ITEMS], F32)
-        slope = tile("slope_b", [P, ITEMS], F32)
-        grad = tile("grad_b", [P, ITEMS], F32)
-        for items in halves:
-            square(tanh2[:, items], sig[:, items], unit_c[:])
-        for items in halves:
-            nc.gpsimd.tensor_scalar(slope[:, items], tanh2[:, items], -1.0, 1.0, ALU.mult, ALU.add)
-        for items in halves:
-            nc.gpsimd.tensor_tensor(grad[:, items], scaled[B][:, items], slope[:, items], ALU.mult)
-        nc.vector.tensor_copy(result[B][:].indirect(offsets[:]), grad[:])
-        store_plane(B)
-        pool_round(A, 1, unit_tile("unit0", "slope_b"))
+        for turn, t in ((1, B), (2, C)):
+            sig = gather(t, "turn%d" % turn)
+            tanh2 = tile("tanh2_%d" % t, [P, ITEMS], F32)
+            for items in halves if t == B else (whole,):
+                nc.scalar.activation(out=tanh2[:, items], in_=sig[:, items], func=ACT.Square, scale=2.0, bias=-1.0)
+            for items in halves if t == B else (whole,):
+                nc.gpsimd.tensor_scalar(slopes[t][:, items], tanh2[:, items], -1.0, 1.0, ALU.mult, ALU.add)
+            for items in halves if t == B else (linked,):
+                nc.gpsimd.tensor_tensor(grads[t][:, items], scaled[t][:, items], slopes[t][:, items], ALU.mult)
+            if t == B:
+                nc.vector.tensor_copy(window(B, whole), grads[B][:, whole])
+                store_plane(B)
+        pool_round(A, 0, CHUNK, units[C])
 
-        sig = gather(C)
-        tanh2 = tile("tanh2_c", [P, ITEMS], F32)
-        slope = tile("slope_c", [P, ITEMS], F32)
-        grad_c = tile("grad_c", [P, ITEMS], F32)
-        for items in halves:
-            square(tanh2[:, items], sig[:, items], unit_c[:])
-        for items in halves:
-            nc.scalar.activation(out=slope[:, items], in_=tanh2[:, items], func=ACT.Identity, scale=-1.0, bias=unit_c[:])
-        for h, items in enumerate(halves):
-            nc.gpsimd.tensor_tensor(grad_c[:, items], scaled_c[h][:], slope[:, items], ALU.mult)
-        pool_round(A, 0, unit_tile("unit1", "slope_c"), 0, GAP)
-
-        sig = gather(D)
-        tanh2 = tile("tanh2_d", [P, ITEMS], F32)
-        slope = tile("slope_d", [P, ITEMS], F32)
-        grad = tile("grad_d", [P, ITEMS], F32)
-        square(tanh2[:, halves[0]], sig[:, halves[0]], one)
-        square(tanh2[:, halves[1]], sig[:, halves[1]], unit_c[:])
-        for items in halves:
-            nc.gpsimd.tensor_scalar(
-                slope[:, items], tanh2[:, items], factors[:, 0:1], weights[:, D : D + 1], ALU.mult, ALU.add
-            )
-        nc.scalar.activation(out=result[C][:].indirect(offsets[:]), in_=grad_c[:], func=ACT.Copy)
+        sig = gather(D, "turn3")
+        nc.scalar.activation(
+            out=slopes[D][:, whole], in_=sig[:], func=ACT.Square, scale=-2.0, bias=result[C][:, COLUMNS : COLUMNS + 1]
+        )
+        nc.scalar.activation(out=window(C, whole), in_=grads[C][:, whole], func=ACT.Copy)
         store_plane(C)
-        for items in halves:
-            nc.vector.tensor_tensor(grad[:, items], slope[:, items], sums[D][:, items], ALU.mult)
-        nc.vector.tensor_copy(result[D][:].indirect(offsets[:]), grad[:])
+        nc.vector.scalar_tensor_tensor(
+            grads[D][:, linked], slopes[D][:, linked], units[C], scaled[D][:, linked], ALU.subtract, ALU.mult
+        )
+        nc.vector.tensor_copy(window(D, whole), grads[D][:, whole])
         store_plane(D)
 
-        unit = unit_tile("unit2", "tanh2_d")
-        pool_round(A, 2, unit)
-        pool_round(A, 3, unit)
-        pool_round(A, 0, unit, GAP, CHUNK)
-        for c in (2, 3, 0):
-            pool_round(B, c, unit)
-
-        def scalar_round(t, c, last=CHUNK):
-            out, source = spot(t, c, 0, last)
-            nc.scalar.copy(out=out, in_=source)
-
-        scalar_round(C, 2)
-        scalar_round(C, 3, CHUNK + 1)
-        scalar_round(C, 0)
-        scalar_round(C, 1)
-        one_bf = pairs[3][:, C // 2, CHUNK : CHUNK + 1, C % 2]
-
-        def vector_round(t, c):
-            out, source = spot(t, c)
-            nc.vector.tensor_scalar(out, source, one_bf, None, ALU.mult)
+        pool_round(A, CHUNK, 2 * CHUNK, units[D])
+        pool_round(B, 2 * CHUNK, 2 * CHUNK + POOL_B, units[D])
+        pool_round(A, 2 * CHUNK, COLUMNS + 1, units[D])
+        scalar_round(C, 2 * CHUNK, COLUMNS + 1)
+        scalar_round(C, 0, CHUNK)
+        scalar_round(C, CHUNK, 2 * CHUNK)
+        after = {t: spot(t, COLUMNS, COLUMNS + 1)[0] for t in (A, C)}
 
         woven = [tile("woven%d" % c, [P, CHUNK, LANES], BF16) for c in range(4)]
         codes = tile("codes", [P, COLUMNS], U32)
@@ -230,9 +216,11 @@ def tile_attend_ghash_tnh_pl_kernel(tc, W, dz, eT, cd, offs, out_0, out_1, out_2
         scales_out = out_2[0].bitcast(I32).rearrange("r (a c) -> a r c", a=4)
 
         def weave(engine_copy, dtype, c, first, last):
-            words_in = pairs[c][:].rearrange("p u c e -> p u (c e)").bitcast(dtype)
+            pairs, start = home(c * CHUNK)
+            skip = c * CHUNK - start
+            words_in = pairs[:].bitcast(dtype).rearrange("p (u c) -> p u c", u=2)
             words = woven[c][:].rearrange("p c t -> p (c t)").bitcast(dtype).rearrange("p (c u) -> p c u", u=2)
-            engine_copy(out=words[:, first:last, :], in_=words_in[:, :, first:last].rearrange("p u c -> p c u"))
+            engine_copy(out=words[:, first:last, :], in_=words_in[:, :, skip + first : skip + last].rearrange("p u c -> p c u"))
 
         def quantise(c, first, last):
             nc.vector.quantize_mx(
@@ -244,20 +232,18 @@ def tile_attend_ghash_tnh_pl_kernel(tc, W, dz, eT, cd, offs, out_0, out_1, out_2
         def store_words(queue, first, last):
             queue.dma_start(out=words_out[:, first:last], in_=codes[:, first:last].bitcast(I32))
 
-        vector_round(D, 2)
-        vector_round(D, 3)
-        scalar_round(D, 0)
-        scalar_round(D, 1)
+        vector_round(D, 2 * CHUNK, COLUMNS, after[C], 1.0)
+        vector_round(B, 2 * CHUNK + POOL_B, COLUMNS, after[A], 1.0)
+        vector_round(B, 0, CHUNK, after[A], 1.0)
+        scalar_round(D, 0, CHUNK)
+        scalar_round(D, CHUNK, 2 * CHUNK)
         weave(nc.vector.tensor_copy, I32, 2, 0, CHUNK)
+        vector_round(B, CHUNK, 2 * CHUNK, after[A], 1.0)
         weave(nc.vector.tensor_copy, I32, 3, 0, CHUNK)
-        vector_round(B, 1)
-        quantise(2, 0, CHUNK)
-        store_words(nc.sync, 2 * CHUNK, 3 * CHUNK)
-        weave(nc.vector.tensor_copy, I32, 0, 0, CHUNK)
-        quantise(3, 0, CHUNK)
-        store_words(nc.sync, 3 * CHUNK, 4 * CHUNK)
-        quantise(0, 0, CHUNK)
-        store_words(nc.sync, 0, CHUNK)
+        weave(nc.scalar.copy, F32, 0, 0, CHUNK)
+        for c in (2, 3, 0):
+            quantise(c, 0, CHUNK)
+            store_words(nc.sync, c * CHUNK, (c + 1) * CHUNK)
         for first in (0, HALF):
             weave(nc.scalar.copy, F32, 1, first, first + HALF)
             quantise(1, first, first + HALF)

@@ -20,10 +20,9 @@ FEATURES = 512
 COLUMNS = 2048
 CHUNK = 512
 HALF = 256
-LINK = 32
 SPARE = 8
-ORDER = (2, 3, 0, 1)
-POOL_B = 320
+ORDER = (2, 0, 3, 1)
+POOL_C = 256
 FLOPS = 2 * 512 * 512 * 512
 
 
@@ -42,8 +41,8 @@ def tile_attend_ghash_tnh_pl_kernel(tc, W, dz, eT, cd, offs, out_0, out_1, out_2
         w_raw = tile("w_raw", [P, LANES, FEATURES], F32)
         table = [tile("table%d" % t, [P, COLUMNS], F32) for t in range(LANES)]
         A, B, C, D = ORDER
-        result = {t: tile("result%d" % t, [P, COLUMNS + SPARE], F32) for t in (A, C)}
-        result[B] = tile("result%d" % B, [P, COLUMNS], F32)
+        result = {t: tile("result%d" % t, [P, COLUMNS + SPARE], F32) for t in (B, C)}
+        result[A] = tile("result%d" % A, [P, COLUMNS], F32)
 
         eT_rows = eT.rearrange("(p t) c -> p t c", t=LANES)
         out_rows = out_0.rearrange("(p t) c -> p t c", t=LANES)
@@ -57,11 +56,9 @@ def tile_attend_ghash_tnh_pl_kernel(tc, W, dz, eT, cd, offs, out_0, out_1, out_2
 
         warm = tile("warm", [P, 1], F32)
         nc.scalar.activation(out=warm[:], in_=weights[:, 0:1], func=ACT.Sigmoid)
-        minus_half = tile("minus_half", [P, 1], F32)
-        nc.vector.memset(minus_half[:], -0.5)
         for t in ORDER[:2]:
             nc.vector.memset(result[t][:, :COLUMNS].bitcast(I32), 0)
-        nc.vector.memset(result[A][:, COLUMNS:], 1.0)
+        nc.vector.memset(result[B][:, COLUMNS:], 1.0)
         nc.gpsimd.memset(result[C][:, :COLUMNS], 0.0)
         nc.gpsimd.memset(result[C][:, COLUMNS:], 1.0)
 
@@ -113,13 +110,12 @@ def tile_attend_ghash_tnh_pl_kernel(tc, W, dz, eT, cd, offs, out_0, out_1, out_2
         whole = slice(0, ITEMS)
         extra = slice(ITEMS, ITEMS + SPARE)
         linked = slice(0, ITEMS + 1)
-        halves = (slice(0, HALF), slice(HALF, ITEMS))
         scaled = {t: tile("scaled%d" % t, [P, ITEMS + SPARE], F32) for t in ORDER}
-        factor = {A: -4.0, B: 1.0, C: 1.0, D: -1.0}
+        factor = {A: -4.0, B: -1.0, C: -1.0, D: -1.0}
         slopes = {t: tile("slope%d" % t, [P, ITEMS + SPARE], F32) for t in ORDER}
         for t in (C, D):
             nc.vector.memset(scaled[t][:, extra], factor[t])
-            nc.vector.memset(slopes[t][:, extra], 0.0 if t == D else 1.0)
+            nc.vector.memset(slopes[t][:, extra], 0.0)
         for t in ORDER:
             nc.vector.tensor_scalar(scaled[t][:, whole], sums[t][:], weights[:, t : t + 1], factor[t], ALU.mult, ALU.mult)
 
@@ -162,52 +158,43 @@ def tile_attend_ghash_tnh_pl_kernel(tc, W, dz, eT, cd, offs, out_0, out_1, out_2
         grads = {t: tile("grad%d" % t, [P, ITEMS + SPARE], F32) for t in ORDER}
         units = {t: grads[t][:, ITEMS : ITEMS + 1] for t in ORDER}
 
-        sig, slope, grad = gather(A, "sig_first"), slopes[A], grads[A]
-        early, late = halves
-        square = tile("square", [P, ITEMS], F32)
-        own, shared = slice(0, HALF - LINK), slice(HALF - LINK, HALF)
-        squared = slice(shared.start, ITEMS)
-        nc.scalar.activation(out=square[:, squared], in_=sig[:, squared], func=ACT.Square, bias=minus_half[:])
-        nc.vector.scalar_tensor_tensor(slope[:, own], sig[:, own], 1.0, sig[:, own], ALU.subtract, ALU.mult)
-        nc.vector.tensor_scalar(slope[:, shared], square[:, shared], 0.25, None, ALU.subtract)
-        nc.vector.scalar_tensor_tensor(grad[:, late], square[:, late], 0.25, scaled[A][:, late], ALU.subtract, ALU.mult)
-        nc.vector.tensor_tensor(window(A, early), scaled[A][:, early], slope[:, early], ALU.mult)
-        nc.vector.tensor_copy(window(A, late), grad[:, late])
+        def square(t, sig, bias):
+            nc.scalar.activation(out=slopes[t][:, whole], in_=sig[:], func=ACT.Square, scale=-2.0, bias=bias)
+
+        def product(t, items):
+            nc.vector.scalar_tensor_tensor(
+                grads[t][:, items], slopes[t][:, items], 1.0, scaled[t][:, items], ALU.subtract, ALU.mult
+            )
+
+        sig = gather(A, "sig_a")
+        nc.vector.scalar_tensor_tensor(slopes[A][:, whole], sig[:], 1.0, sig[:], ALU.subtract, ALU.mult)
+        nc.vector.tensor_tensor(window(A, whole), scaled[A][:, whole], slopes[A][:, whole], ALU.mult)
         store_plane(A)
 
-        for turn, t in ((1, B), (2, C)):
-            sig = gather(t, "turn%d" % turn)
-            tanh2 = tile("tanh2_%d" % t, [P, ITEMS], F32)
-            for items in halves if t == B else (whole,):
-                nc.scalar.activation(out=tanh2[:, items], in_=sig[:, items], func=ACT.Square, scale=2.0, bias=-1.0)
-            for items in halves if t == B else (whole,):
-                nc.gpsimd.tensor_scalar(slopes[t][:, items], tanh2[:, items], -1.0, 1.0, ALU.mult, ALU.add)
-            for items in halves if t == B else (linked,):
-                nc.gpsimd.tensor_tensor(grads[t][:, items], scaled[t][:, items], slopes[t][:, items], ALU.mult)
-            if t == B:
-                nc.vector.tensor_copy(window(B, whole), grads[B][:, whole])
-                store_plane(B)
-        pool_round(A, 0, CHUNK, units[C])
-
-        sig = gather(D, "turn3")
-        nc.scalar.activation(
-            out=slopes[D][:, whole], in_=sig[:], func=ACT.Square, scale=-2.0, bias=result[C][:, COLUMNS : COLUMNS + 1]
-        )
-        nc.scalar.activation(out=window(C, whole), in_=grads[C][:, whole], func=ACT.Copy)
+        square(B, gather(B, "sig_b"), 1.0)
+        product(B, whole)
+        square(C, gather(C, "sig_c"), 1.0)
+        product(C, linked)
+        nc.vector.tensor_copy(window(C, whole), grads[C][:, whole])
         store_plane(C)
-        nc.vector.scalar_tensor_tensor(
-            grads[D][:, linked], slopes[D][:, linked], units[C], scaled[D][:, linked], ALU.subtract, ALU.mult
-        )
+        pool_round(A, 2 * CHUNK, COLUMNS, units[C])
+        pool_round(A, 0, CHUNK, units[C])
+        pool_round(A, CHUNK, 2 * CHUNK, units[C])
+
+        square(D, gather(D, "sig_d"), result[B][:, COLUMNS : COLUMNS + 1])
+        nc.scalar.activation(out=window(B, whole), in_=grads[B][:, whole], func=ACT.Copy)
+        store_plane(B)
+        product(D, linked)
         nc.vector.tensor_copy(window(D, whole), grads[D][:, whole])
         store_plane(D)
 
-        pool_round(A, CHUNK, 2 * CHUNK, units[D])
-        pool_round(B, 2 * CHUNK, 2 * CHUNK + POOL_B, units[D])
-        pool_round(A, 2 * CHUNK, COLUMNS + 1, units[D])
-        scalar_round(C, 2 * CHUNK, COLUMNS + 1)
-        scalar_round(C, 0, CHUNK)
-        scalar_round(C, CHUNK, 2 * CHUNK)
-        after = {t: spot(t, COLUMNS, COLUMNS + 1)[0] for t in (A, C)}
+        pool_round(C, 0, CHUNK, units[D])
+        pool_round(C, CHUNK, CHUNK + POOL_C, units[D])
+        pool_round(C, 2 * CHUNK, COLUMNS + 1, units[D])
+        scalar_round(B, 2 * CHUNK, COLUMNS + 1)
+        scalar_round(B, 0, CHUNK)
+        scalar_round(B, CHUNK, 2 * CHUNK)
+        after = {t: spot(t, COLUMNS, COLUMNS + 1)[0] for t in (B, C)}
 
         woven = [tile("woven%d" % c, [P, CHUNK, LANES], BF16) for c in range(4)]
         codes = tile("codes", [P, COLUMNS], U32)
@@ -232,13 +219,11 @@ def tile_attend_ghash_tnh_pl_kernel(tc, W, dz, eT, cd, offs, out_0, out_1, out_2
         def store_words(queue, first, last):
             queue.dma_start(out=words_out[:, first:last], in_=codes[:, first:last].bitcast(I32))
 
-        vector_round(D, 2 * CHUNK, COLUMNS, after[C], 1.0)
-        vector_round(B, 2 * CHUNK + POOL_B, COLUMNS, after[A], 1.0)
-        vector_round(B, 0, CHUNK, after[A], 1.0)
+        vector_round(D, 2 * CHUNK, COLUMNS, after[B], 1.0)
+        vector_round(C, CHUNK + POOL_C, 2 * CHUNK, after[C], 1.0)
         scalar_round(D, 0, CHUNK)
         scalar_round(D, CHUNK, 2 * CHUNK)
         weave(nc.vector.tensor_copy, I32, 2, 0, CHUNK)
-        vector_round(B, CHUNK, 2 * CHUNK, after[A], 1.0)
         weave(nc.vector.tensor_copy, I32, 3, 0, CHUNK)
         weave(nc.scalar.copy, F32, 0, 0, CHUNK)
         for c in (2, 3, 0):

@@ -21,8 +21,7 @@ COLUMNS = 2048
 CHUNK = 512
 HALF = 256
 SPARE = 8
-ORDER = (2, 0, 3, 1)
-POOL_C = 256
+ORDER = (2, 0, 1, 3)
 FLOPS = 2 * 512 * 512 * 512
 
 
@@ -41,8 +40,8 @@ def tile_attend_ghash_tnh_pl_kernel(tc, W, dz, eT, cd, offs, out_0, out_1, out_2
         w_raw = tile("w_raw", [P, LANES, FEATURES], F32)
         table = [tile("table%d" % t, [P, COLUMNS], F32) for t in range(LANES)]
         A, B, C, D = ORDER
-        result = {t: tile("result%d" % t, [P, COLUMNS + SPARE], F32) for t in (B, C)}
-        result[A] = tile("result%d" % A, [P, COLUMNS], F32)
+        result = {t: tile("result%d" % t, [P, COLUMNS + SPARE], F32) for t in (A, B)}
+        result[C] = tile("result%d" % C, [P, COLUMNS], F32)
 
         eT_rows = eT.rearrange("(p t) c -> p t c", t=LANES)
         out_rows = out_0.rearrange("(p t) c -> p t c", t=LANES)
@@ -58,9 +57,9 @@ def tile_attend_ghash_tnh_pl_kernel(tc, W, dz, eT, cd, offs, out_0, out_1, out_2
         nc.scalar.activation(out=warm[:], in_=weights[:, 0:1], func=ACT.Sigmoid)
         for t in ORDER[:2]:
             nc.vector.memset(result[t][:, :COLUMNS].bitcast(I32), 0)
-        nc.vector.memset(result[B][:, COLUMNS:], 1.0)
-        nc.gpsimd.memset(result[C][:, :COLUMNS], 0.0)
-        nc.gpsimd.memset(result[C][:, COLUMNS:], 1.0)
+        for t in (A, B):
+            nc.vector.memset(result[t][:, COLUMNS:], 1.0)
+        nc.gpsimd.memset(result[C][:], 0.0)
 
         dz_bf = [tile("dz_bf%d" % h, [P, HALF, LANES], BF16) for h in range(2)]
         dz_codes = tile("dz_codes", [P, ITEMS], U32)
@@ -161,9 +160,9 @@ def tile_attend_ghash_tnh_pl_kernel(tc, W, dz, eT, cd, offs, out_0, out_1, out_2
         def square(t, sig, bias):
             nc.scalar.activation(out=slopes[t][:, whole], in_=sig[:], func=ACT.Square, scale=-2.0, bias=bias)
 
-        def product(t, items):
+        def product(t, items, unit):
             nc.vector.scalar_tensor_tensor(
-                grads[t][:, items], slopes[t][:, items], 1.0, scaled[t][:, items], ALU.subtract, ALU.mult
+                grads[t][:, items], slopes[t][:, items], unit, scaled[t][:, items], ALU.subtract, ALU.mult
             )
 
         sig = gather(A, "sig_a")
@@ -172,29 +171,25 @@ def tile_attend_ghash_tnh_pl_kernel(tc, W, dz, eT, cd, offs, out_0, out_1, out_2
         store_plane(A)
 
         square(B, gather(B, "sig_b"), 1.0)
-        product(B, whole)
+        product(B, whole, 1.0)
         square(C, gather(C, "sig_c"), 1.0)
-        product(C, linked)
+        product(C, linked, 1.0)
         nc.vector.tensor_copy(window(C, whole), grads[C][:, whole])
         store_plane(C)
-        pool_round(A, 2 * CHUNK, COLUMNS, units[C])
-        pool_round(A, 0, CHUNK, units[C])
         pool_round(A, CHUNK, 2 * CHUNK, units[C])
+        pool_round(A, 2 * CHUNK, COLUMNS + 1, units[C])
 
         square(D, gather(D, "sig_d"), result[B][:, COLUMNS : COLUMNS + 1])
         nc.scalar.activation(out=window(B, whole), in_=grads[B][:, whole], func=ACT.Copy)
         store_plane(B)
-        product(D, linked)
-        nc.vector.tensor_copy(window(D, whole), grads[D][:, whole])
+        product(D, linked, spot(A, COLUMNS, COLUMNS + 1)[0])
+        nc.scalar.activation(out=window(D, whole), in_=grads[D][:, whole], func=ACT.Copy)
         store_plane(D)
 
-        pool_round(C, 0, CHUNK, units[D])
-        pool_round(C, CHUNK, CHUNK + POOL_C, units[D])
-        pool_round(C, 2 * CHUNK, COLUMNS + 1, units[D])
-        scalar_round(B, 2 * CHUNK, COLUMNS + 1)
-        scalar_round(B, 0, CHUNK)
-        scalar_round(B, CHUNK, 2 * CHUNK)
-        after = {t: spot(t, COLUMNS, COLUMNS + 1)[0] for t in (B, C)}
+        vector_round(A, 0, CHUNK, units[D], 1.0)
+        for t in (C, B):
+            for first, last in ((0, CHUNK), (CHUNK, 2 * CHUNK), (2 * CHUNK, COLUMNS)):
+                vector_round(t, first, last, units[D], 1.0)
 
         woven = [tile("woven%d" % c, [P, CHUNK, LANES], BF16) for c in range(4)]
         codes = tile("codes", [P, COLUMNS], U32)
@@ -219,20 +214,19 @@ def tile_attend_ghash_tnh_pl_kernel(tc, W, dz, eT, cd, offs, out_0, out_1, out_2
         def store_words(queue, first, last):
             queue.dma_start(out=words_out[:, first:last], in_=codes[:, first:last].bitcast(I32))
 
-        vector_round(D, 2 * CHUNK, COLUMNS, after[B], 1.0)
-        vector_round(C, CHUNK + POOL_C, 2 * CHUNK, after[C], 1.0)
-        scalar_round(D, 0, CHUNK)
-        scalar_round(D, CHUNK, 2 * CHUNK)
-        weave(nc.vector.tensor_copy, I32, 2, 0, CHUNK)
-        weave(nc.vector.tensor_copy, I32, 3, 0, CHUNK)
-        weave(nc.scalar.copy, F32, 0, 0, CHUNK)
-        for c in (2, 3, 0):
+        for c in range(2):
+            vector_round(D, c * CHUNK, (c + 1) * CHUNK, units[D], 1.0)
+        scalar_round(D, 2 * CHUNK, COLUMNS)
+        for c in range(2):
+            weave(nc.vector.tensor_copy, I32, c, 0, CHUNK)
+        weave(nc.scalar.copy, F32, 2, 0, CHUNK)
+        for c in range(3):
             quantise(c, 0, CHUNK)
             store_words(nc.sync, c * CHUNK, (c + 1) * CHUNK)
-        for first in (0, HALF):
-            weave(nc.scalar.copy, F32, 1, first, first + HALF)
-            quantise(1, first, first + HALF)
-        store_words(nc.scalar, CHUNK, 2 * CHUNK)
+        for first, queue in ((0, nc.sync), (HALF, nc.scalar)):
+            weave(nc.scalar.copy, F32, 3, first, first + HALF)
+            quantise(3, first, first + HALF)
+            store_words(queue, 3 * CHUNK + first, 3 * CHUNK + first + HALF)
         for q in range(4):
             queue = nc.sync if q % 2 == 0 else nc.scalar
             queue.dma_start(out=scales_out[:, 4 * q : 4 * q + 4, :], in_=scales[32 * q : 32 * q + 16, :].bitcast(I32))

@@ -21,6 +21,8 @@ COLUMNS = 2048
 CHUNK = 512
 HALF = 256
 SPARE = 8
+SHARE = 128
+SPLIT = 768
 ORDER = (2, 0, 1, 3)
 FLOPS = 2 * 512 * 512 * 512
 
@@ -118,18 +120,11 @@ def tile_attend_ghash_tnh_pl_kernel(tc, W, dz, eT, cd, offs, out_0, out_1, out_2
         for t in ORDER:
             nc.vector.tensor_scalar(scaled[t][:, whole], sums[t][:], weights[:, t : t + 1], factor[t], ALU.mult, ALU.mult)
 
-        back = tile("back", [P, 4 * (2 * CHUNK + SPARE)], BF16)
-        front = [tile("front%d" % c, [P, 4 * CHUNK], BF16) for c in range(2)]
-
-        def home(first):
-            if first >= 2 * CHUNK:
-                return back, 2 * CHUNK
-            return front[first // CHUNK], first // CHUNK * CHUNK
+        pairs = tile("pairs", [P, 4 * (COLUMNS + SPARE)], BF16)
 
         def spot(t, first, last):
-            pairs, start = home(first)
-            base = t // 2 * (pairs.shape[1] // 2) + t % 2
-            return pairs[:, base + 2 * (first - start) : base + 2 * (last - start) - 1 : 2], result[t][:, first:last]
+            base = t // 2 * 2 * (COLUMNS + SPARE) + t % 2
+            return pairs[:, base + 2 * first : base + 2 * last - 1 : 2], result[t][:, first:last]
 
         def pool_round(t, first, last, unit):
             out, source = spot(t, first, last)
@@ -176,20 +171,19 @@ def tile_attend_ghash_tnh_pl_kernel(tc, W, dz, eT, cd, offs, out_0, out_1, out_2
         product(C, linked, 1.0)
         nc.vector.tensor_copy(window(C, whole), grads[C][:, whole])
         store_plane(C)
-        pool_round(A, CHUNK, 2 * CHUNK, units[C])
-        pool_round(A, 2 * CHUNK, COLUMNS + 1, units[C])
+        pool_round(A, CHUNK, COLUMNS + 1, units[C])
 
         square(D, gather(D, "sig_d"), result[B][:, COLUMNS : COLUMNS + 1])
         nc.scalar.activation(out=window(B, whole), in_=grads[B][:, whole], func=ACT.Copy)
         store_plane(B)
         product(D, linked, spot(A, COLUMNS, COLUMNS + 1)[0])
-        nc.scalar.activation(out=window(D, whole), in_=grads[D][:, whole], func=ACT.Copy)
+        nc.vector.tensor_copy(window(D, slice(0, SHARE)), grads[D][:, :SHARE])
+        nc.scalar.activation(out=window(D, slice(SHARE, ITEMS)), in_=grads[D][:, SHARE:ITEMS], func=ACT.Copy)
         store_plane(D)
 
         vector_round(A, 0, CHUNK, units[D], 1.0)
         for t in (C, B):
-            for first, last in ((0, CHUNK), (CHUNK, 2 * CHUNK), (2 * CHUNK, COLUMNS)):
-                vector_round(t, first, last, units[D], 1.0)
+            vector_round(t, 0, COLUMNS, units[D], 1.0)
 
         woven = [tile("woven%d" % c, [P, CHUNK, LANES], BF16) for c in range(4)]
         codes = tile("codes", [P, COLUMNS], U32)
@@ -198,8 +192,7 @@ def tile_attend_ghash_tnh_pl_kernel(tc, W, dz, eT, cd, offs, out_0, out_1, out_2
         scales_out = out_2[0].bitcast(I32).rearrange("r (a c) -> a r c", a=4)
 
         def weave(engine_copy, dtype, c, first, last):
-            pairs, start = home(c * CHUNK)
-            skip = c * CHUNK - start
+            skip = c * CHUNK
             words_in = pairs[:].bitcast(dtype).rearrange("p (u c) -> p u c", u=2)
             words = woven[c][:].rearrange("p c t -> p (c t)").bitcast(dtype).rearrange("p (c u) -> p c u", u=2)
             engine_copy(out=words[:, first:last, :], in_=words_in[:, :, skip + first : skip + last].rearrange("p u c -> p c u"))
@@ -214,8 +207,9 @@ def tile_attend_ghash_tnh_pl_kernel(tc, W, dz, eT, cd, offs, out_0, out_1, out_2
         def store_words(queue, first, last):
             queue.dma_start(out=words_out[:, first:last], in_=codes[:, first:last].bitcast(I32))
 
-        for c in range(2):
-            vector_round(D, c * CHUNK, (c + 1) * CHUNK, units[D], 1.0)
+        vector_round(D, 0, CHUNK, units[D], 1.0)
+        vector_round(D, CHUNK, SPLIT, units[D], 1.0)
+        scalar_round(D, SPLIT, 2 * CHUNK)
         scalar_round(D, 2 * CHUNK, COLUMNS)
         for c in range(2):
             weave(nc.vector.tensor_copy, I32, c, 0, CHUNK)
@@ -223,10 +217,13 @@ def tile_attend_ghash_tnh_pl_kernel(tc, W, dz, eT, cd, offs, out_0, out_1, out_2
         for c in range(3):
             quantise(c, 0, CHUNK)
             store_words(nc.sync, c * CHUNK, (c + 1) * CHUNK)
-        for first, queue in ((0, nc.sync), (HALF, nc.scalar)):
-            weave(nc.scalar.copy, F32, 3, first, first + HALF)
-            quantise(3, first, first + HALF)
-            store_words(queue, 3 * CHUNK + first, 3 * CHUNK + first + HALF)
+        weave(nc.scalar.copy, F32, 3, 0, HALF)
+        quantise(3, 0, HALF)
+        store_words(nc.sync, 3 * CHUNK, 3 * CHUNK + HALF)
+        for first in (HALF, HALF + HALF // 2):
+            weave(nc.scalar.copy, F32, 3, first, first + HALF // 2)
+            quantise(3, first, first + HALF // 2)
+        store_words(nc.scalar, 3 * CHUNK + HALF, COLUMNS)
         for q in range(4):
             queue = nc.sync if q % 2 == 0 else nc.scalar
             queue.dma_start(out=scales_out[:, 4 * q : 4 * q + 4, :], in_=scales[32 * q : 32 * q + 16, :].bitcast(I32))

@@ -21,8 +21,7 @@ COLUMNS = 2048
 CHUNK = 512
 HALF = 256
 SPARE = 8
-SHARE = 128
-SPLIT = 768
+SPLIT = 1024
 ORDER = (2, 0, 1, 3)
 FLOPS = 2 * 512 * 512 * 512
 
@@ -59,8 +58,8 @@ def tile_attend_ghash_tnh_pl_kernel(tc, W, dz, eT, cd, offs, out_0, out_1, out_2
         nc.scalar.activation(out=warm[:], in_=weights[:, 0:1], func=ACT.Sigmoid)
         for t in ORDER[:2]:
             nc.vector.memset(result[t][:, :COLUMNS].bitcast(I32), 0)
-        for t in (A, B):
-            nc.vector.memset(result[t][:, COLUMNS:], 1.0)
+        for t, value in ((A, 1.0), (B, 2.0)):
+            nc.vector.memset(result[t][:, COLUMNS:], value)
         nc.gpsimd.memset(result[C][:], 0.0)
 
         dz_bf = [tile("dz_bf%d" % h, [P, HALF, LANES], BF16) for h in range(2)]
@@ -114,9 +113,8 @@ def tile_attend_ghash_tnh_pl_kernel(tc, W, dz, eT, cd, offs, out_0, out_1, out_2
         scaled = {t: tile("scaled%d" % t, [P, ITEMS + SPARE], F32) for t in ORDER}
         factor = {A: -4.0, B: -1.0, C: -1.0, D: -1.0}
         slopes = {t: tile("slope%d" % t, [P, ITEMS + SPARE], F32) for t in ORDER}
-        for t in (C, D):
-            nc.vector.memset(scaled[t][:, extra], factor[t])
-            nc.vector.memset(slopes[t][:, extra], 0.0)
+        nc.vector.memset(scaled[C][:, extra], factor[C])
+        nc.vector.memset(slopes[C][:, extra], 0.0)
         for t in ORDER:
             nc.vector.tensor_scalar(scaled[t][:, whole], sums[t][:], weights[:, t : t + 1], factor[t], ALU.mult, ALU.mult)
 
@@ -141,19 +139,21 @@ def tile_attend_ghash_tnh_pl_kernel(tc, W, dz, eT, cd, offs, out_0, out_1, out_2
         def window(t, items):
             return result[t][:].indirect(offsets[:, items.start // 16 : items.stop // 16])
 
-        def gather(t, tag):
-            sig = tile("sig%d" % t, [P, ITEMS], F32, tag)
-            nc.scalar.activation(out=sig[:], in_=table[t][:].indirect(offsets[:]), func=ACT.Sigmoid, scale=2.0)
+        def gather(t, tag, two=2.0):
+            sig = tile("sig%d" % t, [P, ITEMS + SPARE], F32, tag)
+            if t == C:
+                nc.vector.memset(sig[:, extra], 1.0)
+            nc.scalar.activation(out=sig[:, whole], in_=table[t][:].indirect(offsets[:]), func=ACT.Sigmoid, scale=two)
             return sig
 
         def store_plane(t):
             nc.sync.dma_start(out=out_rows[:, t, :], in_=result[t][:, :COLUMNS])
 
         grads = {t: tile("grad%d" % t, [P, ITEMS + SPARE], F32) for t in ORDER}
-        units = {t: grads[t][:, ITEMS : ITEMS + 1] for t in ORDER}
+        unit = grads[C][:, ITEMS + 1 : ITEMS + 2]
 
-        def square(t, sig, bias):
-            nc.scalar.activation(out=slopes[t][:, whole], in_=sig[:], func=ACT.Square, scale=-2.0, bias=bias)
+        def square(t, sig, items):
+            nc.scalar.activation(out=slopes[t][:, items], in_=sig[:, items], func=ACT.Square, scale=-2.0, bias=1.0)
 
         def product(t, items, unit):
             nc.vector.scalar_tensor_tensor(
@@ -161,29 +161,29 @@ def tile_attend_ghash_tnh_pl_kernel(tc, W, dz, eT, cd, offs, out_0, out_1, out_2
             )
 
         sig = gather(A, "sig_a")
-        nc.vector.scalar_tensor_tensor(slopes[A][:, whole], sig[:], 1.0, sig[:], ALU.subtract, ALU.mult)
+        nc.vector.scalar_tensor_tensor(slopes[A][:, whole], sig[:, whole], 1.0, sig[:, whole], ALU.subtract, ALU.mult)
         nc.vector.tensor_tensor(window(A, whole), scaled[A][:, whole], slopes[A][:, whole], ALU.mult)
         store_plane(A)
 
-        square(B, gather(B, "sig_b"), 1.0)
+        square(B, gather(B, "sig_b"), whole)
         product(B, whole, 1.0)
-        square(C, gather(C, "sig_c"), 1.0)
-        product(C, linked, 1.0)
+        square(C, gather(C, "sig_c"), linked)
+        product(C, slice(0, ITEMS + 2), 1.0)
+        vector_round(A, 0, CHUNK, slopes[C][:, ITEMS : ITEMS + 1], 1.0)
         nc.vector.tensor_copy(window(C, whole), grads[C][:, whole])
         store_plane(C)
-        pool_round(A, CHUNK, COLUMNS + 1, units[C])
+        pool_round(A, CHUNK, COLUMNS + 1, unit)
+        after = spot(A, COLUMNS, COLUMNS + 1)[0]
 
-        square(D, gather(D, "sig_d"), result[B][:, COLUMNS : COLUMNS + 1])
+        square(D, gather(D, "sig_d", result[B][:, COLUMNS : COLUMNS + 1]), whole)
         nc.scalar.activation(out=window(B, whole), in_=grads[B][:, whole], func=ACT.Copy)
         store_plane(B)
-        product(D, linked, spot(A, COLUMNS, COLUMNS + 1)[0])
-        nc.vector.tensor_copy(window(D, slice(0, SHARE)), grads[D][:, :SHARE])
-        nc.scalar.activation(out=window(D, slice(SHARE, ITEMS)), in_=grads[D][:, SHARE:ITEMS], func=ACT.Copy)
+        product(D, whole, after)
+        nc.scalar.activation(out=window(D, whole), in_=grads[D][:, whole], func=ACT.Copy)
         store_plane(D)
 
-        vector_round(A, 0, CHUNK, units[D], 1.0)
         for t in (C, B):
-            vector_round(t, 0, COLUMNS, units[D], 1.0)
+            vector_round(t, 0, COLUMNS, after, 1.0)
 
         woven = [tile("woven%d" % c, [P, CHUNK, LANES], BF16) for c in range(4)]
         codes = tile("codes", [P, COLUMNS], U32)
@@ -207,9 +207,8 @@ def tile_attend_ghash_tnh_pl_kernel(tc, W, dz, eT, cd, offs, out_0, out_1, out_2
         def store_words(queue, first, last):
             queue.dma_start(out=words_out[:, first:last], in_=codes[:, first:last].bitcast(I32))
 
-        vector_round(D, 0, CHUNK, units[D], 1.0)
-        vector_round(D, CHUNK, SPLIT, units[D], 1.0)
-        scalar_round(D, SPLIT, 2 * CHUNK)
+        vector_round(D, 0, CHUNK, after, 1.0)
+        vector_round(D, CHUNK, SPLIT, after, 1.0)
         scalar_round(D, 2 * CHUNK, COLUMNS)
         for c in range(2):
             weave(nc.vector.tensor_copy, I32, c, 0, CHUNK)

from contextlib import ExitStack

import concourse.mybir as mybir

F32 = mybir.dt.float32
BF16 = mybir.dt.bfloat16
I32 = mybir.dt.int32
U32 = mybir.dt.uint32
U16 = mybir.dt.uint16
U8 = mybir.dt.uint8
E4M3 = mybir.dt.float8_e4m3fn_x4
E5M2 = mybir.dt.float8_e5m2_x4
ACT = mybir.ActivationFunctionType
ALU = mybir.AluOpType

P = 128
LANES = 4
ITEMS = 512
FEATURES = 512
COLUMNS = 2048
CHUNK = 512
HALF = 256
SPARE = 8
SPLIT = 1024
ORDER = (2, 0, 1, 3)
FLOPS = 2 * 512 * 512 * 512


def tile_attend_ghash_tnh_pl_kernel(tc, W, dz, eT, cd, offs, out_0, out_1, out_2):
    nc = tc.nc
    with ExitStack() as ctx:
        keep = ctx.enter_context(tc.tile_pool(name="keep", bufs=1))
        psum = ctx.enter_context(tc.psum_pool(name="psum", bufs=1))

        def tile(name, shape, dtype, tag=None):
            return keep.tile(shape, dtype, name=name, tag=tag or name, align_bytes=64)

        offsets = keep.tile([P, ITEMS // 16], U16, name="offsets")
        weights = tile("weights", [P, LANES], F32)
        dz_raw = tile("dz_raw", [P, LANES, ITEMS], F32)
        w_raw = tile("w_raw", [P, LANES, FEATURES], F32)
        table = [tile("table%d" % t, [P, COLUMNS], F32) for t in range(LANES)]
        A, B, C, D = ORDER
        result = {t: tile("result%d" % t, [P, COLUMNS + SPARE], F32) for t in (A, B)}
        result[C] = tile("result%d" % C, [P, COLUMNS], F32)

        eT_rows = eT.rearrange("(p t) c -> p t c", t=LANES)
        out_rows = out_0.rearrange("(p t) c -> p t c", t=LANES)

        nc.sync.dma_start(out=dz_raw[:], in_=dz.rearrange("(p j) i -> p j i", j=LANES))
        nc.sync.dma_start(out=w_raw[:], in_=W.rearrange("(p j) d -> p j d", j=LANES))
        nc.sync.dma_start(offsets[:], offs)
        nc.scalar.dma_start(out=weights[:], in_=cd.rearrange("(p t) o -> p (t o)", t=LANES))
        for t in ORDER:
            nc.sync.dma_start(out=table[t][:], in_=eT_rows[:, t, :])

        warm = tile("warm", [P, 1], F32)
        nc.scalar.activation(out=warm[:], in_=weights[:, 0:1], func=ACT.Sigmoid)
        for t in ORDER[:2]:
            nc.vector.memset(result[t][:, :COLUMNS].bitcast(I32), 0)
        for t, value in ((A, 1.0), (B, 2.0)):
            nc.vector.memset(result[t][:, COLUMNS:], value)
        nc.gpsimd.memset(result[C][:], 0.0)

        dz_bf = [tile("dz_bf%d" % h, [P, HALF, LANES], BF16) for h in range(2)]
        dz_codes = tile("dz_codes", [P, ITEMS], U32)
        dz_scales = tile("dz_scales", [P, ITEMS], U8)
        for h, engine_copy in enumerate((nc.vector.tensor_copy, nc.scalar.copy)):
            engine_copy(
                out=dz_bf[h][:].rearrange("p (c i) j -> p c j i", i=4),
                in_=dz_raw[:, :, h * HALF : (h + 1) * HALF].rearrange("p j (c i) -> p c j i", i=4),
            )
        for h in range(2):
            span = slice(h * HALF, (h + 1) * HALF)
            nc.vector.quantize_mx(
                out=dz_codes[:, span].bitcast(E5M2),
                scales=dz_scales[:, span],
                in_=dz_bf[h][:].rearrange("p i j -> p (i j)"),
            )

        w_codes = tile("w_codes", [P, FEATURES], U32)
        w_scales = tile("w_scales", [P, FEATURES], U8)
        w_dealt = w_raw[:].rearrange("p j (m t) -> p m j t", t=LANES)
        w_bf = [tile("w_bf%d" % h, [P, 2, P, LANES], BF16) for h in range(2)]
        for h, engine_copy in enumerate((nc.scalar.copy, nc.vector.tensor_copy)):
            engine_copy(out=w_bf[h][:].rearrange("p t m j -> p m j t"), in_=w_dealt[:, :, :, 2 * h : 2 * h + 2])
        for h in (1, 0):
            span = slice(2 * h * P, 2 * (h + 1) * P)
            nc.vector.quantize_mx(
                out=w_codes[:, span].bitcast(E4M3),
                scales=w_scales[:, span],
                in_=w_bf[h][:].rearrange("p t m j -> p (t m j)"),
            )

        sums = [psum.tile([P, ITEMS], F32, name="sums%d" % t) for t in range(LANES)]
        for t in ORDER:
            nc.tensor.matmul_mx(
                out=sums[t][:],
                lhsT=w_codes[:, t * P : (t + 1) * P].bitcast(E4M3),
                lhsT_scale=w_scales[:, t * P : (t + 1) * P],
                rhs=dz_codes[:].bitcast(E5M2),
                rhs_scale=dz_scales[:],
                start=True,
                stop=True,
            )

        result[D] = tile("result%d" % D, [P, COLUMNS], F32, "w_bf0")
        nc.gpsimd.memset(result[D][:], 0.0)

        whole = slice(0, ITEMS)
        extra = slice(ITEMS, ITEMS + SPARE)
        linked = slice(0, ITEMS + 1)
        scaled = {t: tile("scaled%d" % t, [P, ITEMS + SPARE], F32) for t in ORDER}
        factor = {A: -4.0, B: -1.0, C: -1.0, D: -1.0}
        slopes = {t: tile("slope%d" % t, [P, ITEMS + SPARE], F32) for t in ORDER}
        nc.vector.memset(scaled[C][:, extra], factor[C])
        nc.vector.memset(slopes[C][:, extra], 0.0)
        for t in ORDER:
            nc.vector.tensor_scalar(scaled[t][:, whole], sums[t][:], weights[:, t : t + 1], factor[t], ALU.mult, ALU.mult)

        pairs = tile("pairs", [P, 4 * (COLUMNS + SPARE)], BF16)

        def spot(t, first, last):
            base = t // 2 * 2 * (COLUMNS + SPARE) + t % 2
            return pairs[:, base + 2 * first : base + 2 * last - 1 : 2], result[t][:, first:last]

        def pool_round(t, first, last, unit):
            out, source = spot(t, first, last)
            nc.gpsimd.tensor_scalar(out, source, unit, -0.0, ALU.mult, ALU.add)

        def scalar_round(t, first, last):
            out, source = spot(t, first, last)
            nc.scalar.copy(out=out, in_=source)

        def vector_round(t, first, last, unit, other):
            out, source = spot(t, first, last)
            nc.vector.tensor_scalar(out, source, unit, other, ALU.mult, ALU.mult)

        def window(t, items):
            return result[t][:].indirect(offsets[:, items.start // 16 : items.stop // 16])

        def gather(t, tag, two=2.0):
            sig = tile("sig%d" % t, [P, ITEMS + SPARE], F32, tag)
            if t == C:
                nc.vector.memset(sig[:, extra], 1.0)
            nc.scalar.activation(out=sig[:, whole], in_=table[t][:].indirect(offsets[:]), func=ACT.Sigmoid, scale=two)
            return sig

        def store_plane(t):
            nc.sync.dma_start(out=out_rows[:, t, :], in_=result[t][:, :COLUMNS])

        grads = {t: tile("grad%d" % t, [P, ITEMS + SPARE], F32) for t in ORDER}
        unit = grads[C][:, ITEMS + 1 : ITEMS + 2]

        def square(t, sig, items):
            nc.scalar.activation(out=slopes[t][:, items], in_=sig[:, items], func=ACT.Square, scale=-2.0, bias=1.0)

        def product(t, items, unit):
            nc.vector.scalar_tensor_tensor(
                grads[t][:, items], slopes[t][:, items], unit, scaled[t][:, items], ALU.subtract, ALU.mult
            )

        sig = gather(A, "sig_a")
        nc.vector.scalar_tensor_tensor(slopes[A][:, whole], sig[:, whole], 1.0, sig[:, whole], ALU.subtract, ALU.mult)
        nc.vector.tensor_tensor(window(A, whole), scaled[A][:, whole], slopes[A][:, whole], ALU.mult)
        store_plane(A)

        square(B, gather(B, "sig_b"), whole)
        product(B, whole, 1.0)
        square(C, gather(C, "sig_c"), linked)
        product(C, slice(0, ITEMS + 2), 1.0)
        vector_round(A, 0, CHUNK, slopes[C][:, ITEMS : ITEMS + 1], 1.0)
        nc.vector.tensor_copy(window(C, whole), grads[C][:, whole])
        store_plane(C)
        pool_round(A, CHUNK, COLUMNS + 1, unit)
        after = spot(A, COLUMNS, COLUMNS + 1)[0]

        square(D, gather(D, "sig_d", result[B][:, COLUMNS : COLUMNS + 1]), whole)
        nc.scalar.activation(out=window(B, whole), in_=grads[B][:, whole], func=ACT.Copy)
        store_plane(B)
        product(D, whole, after)
        nc.scalar.activation(out=window(D, whole), in_=grads[D][:, whole], func=ACT.Copy)
        store_plane(D)

        for t in (C, B):
            vector_round(t, 0, COLUMNS, after, 1.0)

        woven = [tile("woven%d" % c, [P, CHUNK, LANES], BF16) for c in range(4)]
        codes = tile("codes", [P, COLUMNS], U32)
        scales = tile("scales", [P, CHUNK], U8)
        words_out = out_1[0].rearrange("p c l -> p (c l)").bitcast(I32)
        scales_out = out_2[0].bitcast(I32).rearrange("r (a c) -> a r c", a=4)

        def weave(engine_copy, dtype, c, first, last):
            skip = c * CHUNK
            words_in = pairs[:].bitcast(dtype).rearrange("p (u c) -> p u c", u=2)
            words = woven[c][:].rearrange("p c t -> p (c t)").bitcast(dtype).rearrange("p (c u) -> p c u", u=2)
            engine_copy(out=words[:, first:last, :], in_=words_in[:, :, skip + first : skip + last].rearrange("p u c -> p c u"))

        def quantise(c, first, last):
            nc.vector.quantize_mx(
                out=codes[:, c * CHUNK + first : c * CHUNK + last].bitcast(E4M3),
                scales=scales[4 * c : P, first:last],
                in_=woven[c][:, first:last, :].rearrange("p c t -> p (c t)"),
            )

        def store_words(queue, first, last):
            queue.dma_start(out=words_out[:, first:last], in_=codes[:, first:last].bitcast(I32))

        vector_round(D, 0, CHUNK, after, 1.0)
        vector_round(D, CHUNK, SPLIT, after, 1.0)
        scalar_round(D, 2 * CHUNK, COLUMNS)
        for c in range(2):
            weave(nc.vector.tensor_copy, I32, c, 0, CHUNK)
        weave(nc.scalar.copy, F32, 2, 0, CHUNK)
        for c in range(3):
            quantise(c, 0, CHUNK)
            store_words(nc.sync, c * CHUNK, (c + 1) * CHUNK)
        weave(nc.scalar.copy, F32, 3, 0, HALF)
        quantise(3, 0, HALF)
        store_words(nc.sync, 3 * CHUNK, 3 * CHUNK + HALF)
        for first in (HALF, HALF + HALF // 2):
            weave(nc.scalar.copy, F32, 3, first, first + HALF // 2)
            quantise(3, first, first + HALF // 2)
        store_words(nc.scalar, 3 * CHUNK + HALF, COLUMNS)
        for q in range(4):
            queue = nc.sync if q % 2 == 0 else nc.scalar
            queue.dma_start(out=scales_out[:, 4 * q : 4 * q + 4, :], in_=scales[32 * q : 32 * q + 16, :].bitcast(I32))
